import numpy as np
import ml_dtypes


def mxq(x, axis, fmt="e4m3"):
    dtype, down = {"e4m3": (ml_dtypes.float8_e4m3fn, 7), "e5m2": (ml_dtypes.float8_e5m2, 14)}[fmt]
    v = np.moveaxis(np.asarray(x, np.float32).astype(ml_dtypes.bfloat16).astype(np.float64), axis, -1)
    blocks = v.reshape(v.shape[:-1] + (-1, 32))
    amax = np.abs(blocks).max(-1, keepdims=True)
    byte = np.maximum(np.where(amax > 0, np.frexp(amax)[1] - 1 + 127, 0) - down, 1)
    scale = np.exp2(byte - 127.0)
    codes = (blocks / scale).astype(np.float32).astype(dtype).astype(np.float64)
    return np.moveaxis((codes * scale).reshape(v.shape), -1, axis)


WIDE = False


def mx_kscale(k):
    if not WIDE:
        return np.ones(k)
    levels = np.array([10, -10, 5, -5, 0])
    if k % 512:
        return np.exp2(np.random.permutation(np.resize(levels, k // 32))).repeat(32)
    a = np.empty((k // 512, 16))
    for p in range(k // 512):
        a[p, :8] = np.random.permutation(np.resize(levels, 8))
        for g in range(8):
            far = levels[np.abs(levels - a[p, g]) >= 10]
            a[p, g + 8] = far[np.random.randint(len(far))]
    return np.exp2(a.ravel()).repeat(32)


def f64(x):
    return np.asarray(x).astype(np.float64)


def striped(idx):
    return np.tile(idx.reshape(-1, 16).T, (8, 1)).astype(np.uint16)


def unstriped(offs):
    return offs[:16].T.reshape(-1).astype(np.int64)


def pack_weight(w):
    k, n = w.shape
    w = f64(np.asarray(w, np.float32).astype(ml_dtypes.bfloat16)).reshape(k // 32, 32, n)
    amax = np.abs(w).max(1)
    byte = np.clip(np.where(amax > 0, np.frexp(amax)[1] - 1 + 127 - 7, 1), 1, 254)
    scaled = (w * np.exp2(127.0 - byte)[:, None, :]).reshape(k, n).astype(np.float32)
    words = np.ascontiguousarray(scaled.reshape(k // 512, 128, 4, n).transpose(0, 1, 3, 2)).astype(ml_dtypes.float8_e4m3fn).view(np.uint8)
    return words, np.ascontiguousarray(byte.astype(np.uint8).reshape(k // 512, 16, n))


def unpack_weight(words, scales):
    g, p, n, _ = words.shape
    vals = np.ascontiguousarray(words).view(ml_dtypes.float8_e4m3fn).astype(np.float64) * np.repeat(np.exp2(scales.astype(np.float64) - 127.0), 8, axis=1)[..., None]
    return vals.transpose(0, 1, 3, 2).reshape(g * 512, n)


def relu(v):
    return np.maximum(v, 0.0)


K, T, S, H, N = 1536, 1024, 512, 512, 256


def setup_inputs():
    n = np.random.standard_normal
    s = mx_kscale(K)[:, None]
    u = mx_kscale(H)
    packed = pack_weight(n((K, T)) * s)
    return {
        "x_words": packed[0],
        "x_scales": packed[1],
        "w1": (n((K, H)) / np.sqrt(K) / s).astype(np.float32),
        "w3": (n((K, H)) / np.sqrt(K) / s * u).astype(np.float32),
        "w2": (n((H, N)) / np.sqrt(H) / u[:, None]).astype(np.float32),
        "gate": np.tile(np.random.uniform(0.2, 1.0, S), (N, 1)).astype(np.float32),
        "offs": striped(np.sort(np.random.permutation(T)[:S])),
    }


def reference(x_words, x_scales, w1, w3, w2, gate, offs):
    idx = unstriped(offs)
    xq = unpack_weight(x_words, x_scales)[:, idx]
    h = relu(mxq(f64(w1), 0, "e4m3").T @ xq) * (mxq(f64(w3), 0, "e4m3").T @ xq)
    y = mxq(f64(w2), 0, "e4m3").T @ mxq(h, 0, "e4m3")
    out = np.zeros((N, T))
    out[:, idx] = f64(gate) * y
    return out

@@ -1,0 +1,209 @@
+from contextlib import ExitStack
+
+import concourse.mybir as mybir
+from concourse.masks import make_identity
+
+K, T, S, H, N = 1536, 1024, 512, 512, 256
+FLOPS = 2 * S * (2 * K * H + H * N)
+
+F32 = mybir.dt.float32
+BF16 = mybir.dt.bfloat16
+I32 = mybir.dt.int32
+U32 = mybir.dt.uint32
+U16 = mybir.dt.uint16
+U8 = mybir.dt.uint8
+FP8X4 = mybir.dt.float8_e4m3fn_x4
+MULT = mybir.AluOpType.mult
+MAX = mybir.AluOpType.max
+
+P = 128
+PACK = 4
+PASSES = K // (P * PACK)
+GROUPS = S // P
+HALF = H // 2
+LIST_COL = 16
+
+
+def tile_picked_depth_glu_relu_srt_p_kernel(
+    tc, x_words, x_scales, w1, w3, w2, gate, offs, out
+):
+    nc = tc.nc
+    with ExitStack() as ctx:
+        keep = ctx.enter_context(tc.tile_pool(name="keep", bufs=1))
+        psum = ctx.enter_context(tc.psum_pool(name="psum", bufs=1))
+
+        def sb(name, shape, dtype):
+            return keep.tile(shape, dtype, name=name, align_bytes=64)
+
+        def bank(b, shape):
+            return psum.tile(shape, F32, name="bank%d" % b)
+
+        def cast(engine, dst, src):
+            if engine == "scalar":
+                nc.scalar.copy(dst, src)
+            else:
+                nc.vector.tensor_copy(dst, src)
+
+        def quantise(codes, scales, grouped):
+            nc.vector.quantize_mx(out=codes.bitcast(FP8X4), scales=scales, in_=grouped)
+
+        offsets = keep.tile([P, S // LIST_COL], U16, name="offsets")
+        x_scale_rows = sb("x_scale_rows", [P, T], U8)
+        nc.gpsimd.memset(x_scale_rows[:].bitcast(I32), 0)
+        for q in range(4):
+            nc.gpsimd.dma_start(
+                x_scale_rows[32 * q : 32 * q + 4 * PASSES, :].bitcast(I32),
+                x_scales[:, 4 * q : 4 * q + 4, :].bitcast(I32),
+            )
+
+        def load_rows(name, w, o, cols):
+            width = cols.stop - cols.start
+            raw = sb(name, [P, PACK, width], F32)
+            rows = w[o * P * PACK : (o + 1) * P * PACK, cols]
+            nc.sync.dma_start(raw[:], rows.rearrange("(p j) c -> p j c", j=PACK))
+            return raw
+
+        halves = [slice(0, HALF), slice(HALF, H)]
+        w1_raw = []
+        x_all = []
+        for o in range(PASSES):
+            w1_raw.append(load_rows("w1_raw%d" % o, w1, o, slice(0, H)))
+            if o == 0:
+                nc.sync.dma_start(offsets[:], offs)
+            words = sb("x_all%d" % o, [P, T], U32)
+            nc.sync.dma_start(words[:].bitcast(I32), x_words[o].rearrange("p n t -> p (n t)").bitcast(I32))
+            x_all.append(words)
+        w3_raw = [[load_rows("w3_raw%d_%d" % (hf, o), w3, o, halves[hf]) for o in range(PASSES)] for hf in range(2)]
+        w2_raw = load_rows("w2_raw", w2, 0, slice(0, N))
+        gate_sb = sb("gate_sb", [P, S], F32)
+        nc.sync.dma_start(gate_sb[:], gate[0:P, :])
+
+        ident = sb("ident", [P, P], F32)
+        make_identity(nc, ident[:])
+        windows = []
+        for m in range(N // P):
+            window = sb("window%d" % m, [P, T], F32)
+            nc.vector.memset(window[:], 0.0)
+            windows.append(window)
+
+        x_codes = []
+        x_planes = sb("x_planes", [P, S], U8)
+
+        def first_matmul(acc, g, o, codes, scales):
+            tokens = slice(g * P, (g + 1) * P)
+            nc.tensor.matmul_mx(
+                out=acc,
+                lhsT=x_codes[o][:, tokens].bitcast(FP8X4),
+                lhsT_scale=x_planes[4 * o : P, tokens],
+                rhs=codes.bitcast(FP8X4),
+                rhs_scale=scales,
+                start=(o == 0),
+                stop=(o == PASSES - 1),
+            )
+
+        def cast_half(engine, grouped, raw, lo, hi):
+            dst = grouped.rearrange("p (u r e j) -> p r j u e", u=2, e=2, j=PACK)[:, lo:hi]
+            src = raw.rearrange("p j (r u e) -> p r j u e", u=2, e=2)[:, lo:hi]
+            cast(engine, dst, src)
+
+        a_acc = [bank(g, [P, H]) for g in range(GROUPS)]
+        for o in range(PASSES):
+            codes = sb("w1_codes%d" % o, [P, H], U32)
+            scales = sb("w1_scales%d" % o, [P, H], U8)
+            for hf, engine in enumerate(["scalar", "vector"]):
+                grouped = sb("w1_bf%d_%d" % (o, hf), [P, HALF * PACK], BF16)
+                cast_half(engine, grouped[:], w1_raw[o][:, :, halves[hf]], 0, 64)
+                quantise(codes[:, halves[hf]], scales[:, halves[hf]], grouped[:])
+            picked = sb("x_codes%d" % o, [P, S], U32)
+            nc.vector.tensor_copy(picked[:], x_all[o][:].indirect(offsets[:]))
+            x_codes.append(picked)
+            if o == 0:
+                nc.vector.tensor_copy(x_planes[:], x_scale_rows[:].indirect(offsets[:]))
+            for g in range(GROUPS):
+                first_matmul(a_acc[g][:], g, o, codes[:], scales[:])
+        a_sb = [sb("a_sb%d" % g, [P, H], F32) for g in range(GROUPS)]
+        scalar_rows = [[64, 0, 0], [64, 32, 24]]
+
+        h_rows = [sb("h_rows%d" % g, [P, H], BF16) for g in range(GROUPS)]
+        for hf in range(2):
+            b_acc = [bank((GROUPS * (hf + 1) + g) % 8, [P, HALF]) for g in range(GROUPS)]
+            for o in range(PASSES):
+                codes = sb("w3_codes%d_%d" % (hf, o), [P, HALF], U32)
+                scales = sb("w3_scales%d_%d" % (hf, o), [P, HALF], U8)
+                grouped = sb("w3_bf%d_%d" % (hf, o), [P, HALF * PACK], BF16)
+                raw = w3_raw[hf][o]
+                split = scalar_rows[hf][o]
+                if split > 0:
+                    cast_half("scalar", grouped[:], raw[:], 0, split)
+                if split < 64:
+                    cast_half("vector", grouped[:], raw[:], split, 64)
+                if hf == 0 and o == 0:
+                    for g in range(GROUPS):
+                        nc.scalar.copy(a_sb[g][:], a_acc[g][:])
+                quantise(codes[:], scales[:], grouped[:])
+                for g in range(GROUPS):
+                    first_matmul(b_acc[g][:], g, o, codes[:], scales[:])
+            for g in range(GROUPS):
+                nc.vector.scalar_tensor_tensor(
+                    out=h_rows[g][:].rearrange("p (u f c) -> p u f c", u=2, f=2)[:, :, hf, :],
+                    in0=a_sb[g][:, halves[hf]].rearrange("p (u c) -> p u c", u=2),
+                    scalar=0.0,
+                    in1=b_acc[g][:].rearrange("p (u c) -> p u c", u=2),
+                    op0=MAX,
+                    op1=MULT,
+                )
+
+        w2_codes = sb("w2_codes", [P, N], U32)
+        w2_scales = sb("w2_scales", [P, N], U8)
+        for m in range(N // P):
+            cols = slice(m * P, (m + 1) * P)
+            grouped = sb("w2_bf%d" % m, [P, P * PACK], BF16)
+            nc.scalar.copy(
+                grouped[:].rearrange("p (c i j) -> p c j i", i=4, j=PACK),
+                w2_raw[:, :, cols].rearrange("p j (c i) -> p c j i", i=4),
+            )
+            quantise(w2_codes[:, cols], w2_scales[:, cols], grouped[:])
+
+        y_sb = sb("y_sb", [P, N // P, S], F32)
+        for g in range(GROUPS):
+            tokens = slice(g * P, (g + 1) * P)
+            turned = bank(GROUPS + g, [P, 2, P])
+            pairs = h_rows[g][:].bitcast(F32)
+            for u in range(2):
+                nc.tensor.transpose(turned[:, u, :], pairs[:, u * P : (u + 1) * P], ident[:])
+            grouped = sb("h_bf%d" % g, [P, P * PACK], BF16)
+            nc.scalar.copy(
+                grouped[:].bitcast(F32).rearrange("p (r u) -> p r u", u=2),
+                turned[:].rearrange("p u r -> p r u"),
+            )
+            codes = sb("h_codes%d" % g, [P, P], U32)
+            scales = sb("h_scales%d" % g, [P, P], U8)
+            quantise(codes[:], scales[:], grouped[:])
+            y_acc = bank(g, [P, N // P, P])
+            for m in range(N // P):
+                cols = slice(m * P, (m + 1) * P)
+                nc.tensor.matmul_mx(
+                    out=y_acc[:, m, :],
+                    lhsT=w2_codes[:, cols].bitcast(FP8X4),
+                    lhsT_scale=w2_scales[:, cols],
+                    rhs=codes[:].bitcast(FP8X4),
+                    rhs_scale=scales[:],
+                    start=True,
+                    stop=True,
+                )
+            nc.scalar.copy(y_sb[:, :, tokens], y_acc[:])
+
+        def scatter(m, lo, hi):
+            nc.vector.tensor_tensor(
+                windows[m][:].indirect(offsets[:, lo // LIST_COL : hi // LIST_COL]),
+                y_sb[:, m, lo:hi],
+                gate_sb[:, lo:hi],
+                MULT,
+            )
+
+        scatter(0, 0, S // 2)
+        scatter(1, 0, S // 2)
+        scatter(0, S // 2, S)
+        nc.sync.dma_start(out[0:P, :], windows[0][:])
+        scatter(1, S // 2, S)
+        nc.sync.dma_start(out[P : 2 * P, :], windows[1][:])

@@ -50,11 +50,6 @@ def tile_picked_depth_glu_relu_srt_p_kernel(
         offsets = keep.tile([P, S // LIST_COL], U16, name="offsets")
         x_scale_rows = sb("x_scale_rows", [P, T], U8)
         nc.gpsimd.memset(x_scale_rows[:].bitcast(I32), 0)
-        for q in range(4):
-            nc.gpsimd.dma_start(
-                x_scale_rows[32 * q : 32 * q + 4 * PASSES, :].bitcast(I32),
-                x_scales[:, 4 * q : 4 * q + 4, :].bitcast(I32),
-            )
 
         def load_rows(name, w, o, cols):
             width = cols.stop - cols.start
@@ -64,16 +59,27 @@ def tile_picked_depth_glu_relu_srt_p_kernel(
             return raw
 
         halves = [slice(0, HALF), slice(HALF, H)]
-        w1_raw = []
+        w1_raw = [[], []]
+        w3_raw = [[], []]
         x_all = []
         for o in range(PASSES):
-            w1_raw.append(load_rows("w1_raw%d" % o, w1, o, slice(0, H)))
+            w1_raw[0].append(load_rows("w1_raw0_%d" % o, w1, o, halves[0]))
             if o == 0:
                 nc.sync.dma_start(offsets[:], offs)
+            if o == 1:
+                for q in range(4):
+                    nc.sync.dma_start(
+                        x_scale_rows[32 * q : 32 * q + 4 * PASSES, :].bitcast(I32),
+                        x_scales[:, 4 * q : 4 * q + 4, :].bitcast(I32),
+                    )
             words = sb("x_all%d" % o, [P, T], U32)
             nc.sync.dma_start(words[:].bitcast(I32), x_words[o].rearrange("p n t -> p (n t)").bitcast(I32))
             x_all.append(words)
-        w3_raw = [[load_rows("w3_raw%d_%d" % (hf, o), w3, o, halves[hf]) for o in range(PASSES)] for hf in range(2)]
+        w3_raw[0] = [load_rows("w3_raw0_%d" % o, w3, o, halves[0]) for o in range(PASSES)]
+        w1_raw[1] = [load_rows("w1_raw1_%d" % o, w1, o, halves[1]) for o in range(PASSES)]
+        w3_raw[1] = [load_rows("w3_raw1_%d" % o, w3, o, halves[1]) for o in range(PASSES - 1)]
+        quarters = [slice(HALF, HALF + P), slice(HALF + P, H)]
+        w3_last = [load_rows("w3_last%d" % n, w3, PASSES - 1, quarters[n]) for n in range(2)]
         w2_raw = load_rows("w2_raw", w2, 0, slice(0, N))
         gate_sb = sb("gate_sb", [P, S], F32)
         nc.sync.dma_start(gate_sb[:], gate[0:P, :])
@@ -102,75 +108,99 @@ def tile_picked_depth_glu_relu_srt_p_kernel(
             )
 
         def cast_half(engine, grouped, raw, lo, hi):
-            dst = grouped.rearrange("p (u r e j) -> p r j u e", u=2, e=2, j=PACK)[:, lo:hi]
-            src = raw.rearrange("p j (r u e) -> p r j u e", u=2, e=2)[:, lo:hi]
+            dst = grouped.rearrange("p (c i j) -> p c j i", i=4, j=PACK)[:, lo:hi]
+            src = raw.rearrange("p j (c i) -> p c j i", i=4)[:, lo:hi]
             cast(engine, dst, src)
 
-        a_acc = [bank(g, [P, H]) for g in range(GROUPS)]
-        for o in range(PASSES):
-            codes = sb("w1_codes%d" % o, [P, H], U32)
-            scales = sb("w1_scales%d" % o, [P, H], U8)
-            for hf, engine in enumerate(["scalar", "vector"]):
-                grouped = sb("w1_bf%d_%d" % (o, hf), [P, HALF * PACK], BF16)
-                cast_half(engine, grouped[:], w1_raw[o][:, :, halves[hf]], 0, 64)
-                quantise(codes[:, halves[hf]], scales[:, halves[hf]], grouped[:])
-            picked = sb("x_codes%d" % o, [P, S], U32)
-            nc.vector.tensor_copy(picked[:], x_all[o][:].indirect(offsets[:]))
-            x_codes.append(picked)
-            if o == 0:
-                nc.vector.tensor_copy(x_planes[:], x_scale_rows[:].indirect(offsets[:]))
-            for g in range(GROUPS):
-                first_matmul(a_acc[g][:], g, o, codes[:], scales[:])
-        a_sb = [sb("a_sb%d" % g, [P, H], F32) for g in range(GROUPS)]
-        scalar_rows = [[64, 0, 0], [64, 32, 24]]
+        def prepare(name, raw, split):
+            width = raw.shape[2]
+            grouped = sb(name + "_bf", [P, width * PACK], BF16)
+            if split > 0:
+                cast_half("scalar", grouped[:], raw[:], 0, split)
+            if split < width // 4:
+                cast_half("vector", grouped[:], raw[:], split, width // 4)
+            codes = sb(name + "_codes", [P, width], U32)
+            scales = sb(name + "_scales", [P, width], U8)
+            quantise(codes[:], scales[:], grouped[:])
+            return codes, scales
 
+        def gated(g, cols, a_rows, b_acc):
+            nc.vector.scalar_tensor_tensor(
+                out=h_rows[g][:, cols], in0=a_rows, scalar=0.0, in1=b_acc, op0=MAX, op1=MULT
+            )
+
+        W1_SPLIT = [[64, 64, 64], [64, 64, 32]]
+        W3_SPLIT = [[64, 0, 0], [32, 0]]
+        LAST_SPLIT = [0, 20]
         h_rows = [sb("h_rows%d" % g, [P, H], BF16) for g in range(GROUPS)]
-        for hf in range(2):
-            b_acc = [bank((GROUPS * (hf + 1) + g) % 8, [P, HALF]) for g in range(GROUPS)]
+
+        def first_product(hf):
+            a_acc = [bank(g, [P, HALF]) for g in range(GROUPS)]
             for o in range(PASSES):
-                codes = sb("w3_codes%d_%d" % (hf, o), [P, HALF], U32)
-                scales = sb("w3_scales%d_%d" % (hf, o), [P, HALF], U8)
-                grouped = sb("w3_bf%d_%d" % (hf, o), [P, HALF * PACK], BF16)
-                raw = w3_raw[hf][o]
-                split = scalar_rows[hf][o]
-                if split > 0:
-                    cast_half("scalar", grouped[:], raw[:], 0, split)
-                if split < 64:
-                    cast_half("vector", grouped[:], raw[:], split, 64)
-                if hf == 0 and o == 0:
-                    for g in range(GROUPS):
-                        nc.scalar.copy(a_sb[g][:], a_acc[g][:])
-                quantise(codes[:], scales[:], grouped[:])
+                codes, scales = prepare("w1_%d_%d" % (hf, o), w1_raw[hf][o], W1_SPLIT[hf][o])
+                if hf == 0:
+                    picked = sb("x_codes%d" % o, [P, S], U32)
+                    nc.vector.tensor_copy(picked[:], x_all[o][:].indirect(offsets[:]))
+                    x_codes.append(picked)
+                    if o == 0:
+                        nc.vector.tensor_copy(x_planes[:], x_scale_rows[:].indirect(offsets[:]))
                 for g in range(GROUPS):
-                    first_matmul(b_acc[g][:], g, o, codes[:], scales[:])
+                    first_matmul(a_acc[g][:], g, o, codes[:], scales[:])
+            return a_acc
+
+        def evacuate(a_acc, a_sb):
             for g in range(GROUPS):
-                nc.vector.scalar_tensor_tensor(
-                    out=h_rows[g][:].rearrange("p (u f c) -> p u f c", u=2, f=2)[:, :, hf, :],
-                    in0=a_sb[g][:, halves[hf]].rearrange("p (u c) -> p u c", u=2),
-                    scalar=0.0,
-                    in1=b_acc[g][:].rearrange("p (u c) -> p u c", u=2),
-                    op0=MAX,
-                    op1=MULT,
-                )
+                nc.scalar.copy(a_sb[:, g, :], a_acc[g][:])
+
+        a_acc = first_product(0)
+        b_acc = [bank(GROUPS + g, [P, HALF]) for g in range(GROUPS)]
+        a_sb = w3_raw[0][0]
+        for o in range(PASSES):
+            codes, scales = prepare("w3_0_%d" % o, w3_raw[0][o], W3_SPLIT[0][o])
+            if o == 0:
+                evacuate(a_acc, a_sb)
+            for g in range(GROUPS):
+                first_matmul(b_acc[g][:], g, o, codes[:], scales[:])
+        for g in range(GROUPS):
+            gated(g, halves[0], a_sb[:, g, :], b_acc[g][:])
+
+        a_acc = first_product(1)
+        a_sb = w3_raw[1][0]
+        early = []
+        for o in range(PASSES - 1):
+            early.append(prepare("w3_1_%d" % o, w3_raw[1][o], W3_SPLIT[1][o]))
+            if o == 0:
+                evacuate(a_acc, a_sb)
+        b_acc = []
+        for n in range(2):
+            b_acc.append([bank(GROUPS * (1 - n) + g, [P, P]) for g in range(GROUPS)])
+            cols = slice(n * P, (n + 1) * P)
+            for o in range(PASSES - 1):
+                for g in range(GROUPS):
+                    first_matmul(b_acc[n][g][:], g, o, early[o][0][:, cols], early[o][1][:, cols])
+        for n in range(2):
+            codes, scales = prepare("w3_last_%d" % n, w3_last[n], LAST_SPLIT[n])
+            for g in range(GROUPS):
+                first_matmul(b_acc[n][g][:], g, PASSES - 1, codes[:], scales[:])
 
         w2_codes = sb("w2_codes", [P, N], U32)
         w2_scales = sb("w2_scales", [P, N], U8)
-        for m in range(N // P):
-            cols = slice(m * P, (m + 1) * P)
-            grouped = sb("w2_bf%d" % m, [P, P * PACK], BF16)
-            nc.scalar.copy(
-                grouped[:].rearrange("p (c i j) -> p c j i", i=4, j=PACK),
-                w2_raw[:, :, cols].rearrange("p j (c i) -> p c j i", i=4),
-            )
-            quantise(w2_codes[:, cols], w2_scales[:, cols], grouped[:])
+        w2_bf = sb("w2_bf", [P, N * PACK], BF16)
+        nc.scalar.copy(
+            w2_bf[:].rearrange("p (c i j) -> p c j i", i=4, j=PACK),
+            w2_raw[:].rearrange("p j (c i) -> p c j i", i=4),
+        )
+        quantise(w2_codes[:], w2_scales[:], w2_bf[:])
 
         y_sb = sb("y_sb", [P, N // P, S], F32)
         for g in range(GROUPS):
             tokens = slice(g * P, (g + 1) * P)
+            for n in range(2):
+                gated(g, quarters[n], a_sb[:, g, n * P : (n + 1) * P], b_acc[n][g][:])
             turned = bank(GROUPS + g, [P, 2, P])
             pairs = h_rows[g][:].bitcast(F32)
             for u in range(2):
-                nc.tensor.transpose(turned[:, u, :], pairs[:, u * P : (u + 1) * P], ident[:])
+                nc.tensor.transpose(turned[:, u, :], pairs[:, u : 2 * P : 2], ident[:])
             grouped = sb("h_bf%d" % g, [P, P * PACK], BF16)
             nc.scalar.copy(
                 grouped[:].bitcast(F32).rearrange("p (r u) -> p r u", u=2),
@@ -201,8 +231,9 @@ def tile_picked_depth_glu_relu_srt_p_kernel(
                 MULT,
             )
 
-        scatter(0, 0, S // 2)
-        scatter(1, 0, S // 2)
+        for g in range(2):
+            scatter(0, g * P, (g + 1) * P)
+            scatter(1, g * P, (g + 1) * P)
         scatter(0, S // 2, S)
         nc.sync.dma_start(out[0:P, :], windows[0][:])
         scatter(1, S // 2, S)

@@ -1,7 +1,6 @@
 from contextlib import ExitStack
 
 import concourse.mybir as mybir
-from concourse.masks import make_identity
 
 K, T, S, H, N = 1536, 1024, 512, 512, 256
 FLOPS = 2 * S * (2 * K * H + H * N)
@@ -14,13 +13,14 @@ U16 = mybir.dt.uint16
 U8 = mybir.dt.uint8
 FP8X4 = mybir.dt.float8_e4m3fn_x4
 MULT = mybir.AluOpType.mult
-MAX = mybir.AluOpType.max
+ADD = mybir.AluOpType.add
+RELU = mybir.ActivationFunctionType.Relu
+COPY = mybir.ActivationFunctionType.Copy
 
 P = 128
 PACK = 4
 PASSES = K // (P * PACK)
 GROUPS = S // P
-HALF = H // 2
 LIST_COL = 16
 
 
@@ -38,12 +38,6 @@ def tile_picked_depth_glu_relu_srt_p_kernel(
         def bank(b, shape):
             return psum.tile(shape, F32, name="bank%d" % b)
 
-        def cast(engine, dst, src):
-            if engine == "scalar":
-                nc.scalar.copy(dst, src)
-            else:
-                nc.vector.tensor_copy(dst, src)
-
         def quantise(codes, scales, grouped):
             nc.vector.quantize_mx(out=codes.bitcast(FP8X4), scales=scales, in_=grouped)
 
@@ -51,41 +45,32 @@ def tile_picked_depth_glu_relu_srt_p_kernel(
         x_scale_rows = sb("x_scale_rows", [P, T], U8)
         nc.gpsimd.memset(x_scale_rows[:].bitcast(I32), 0)
 
-        def load_rows(name, w, o, cols):
-            width = cols.stop - cols.start
-            raw = sb(name, [P, PACK, width], F32)
+        def raw_slot(slot, shape):
+            return keep.tile(shape, F32, name="raw%d" % slot, align_bytes=64)
+
+        def load_rows(raw, w, o, cols):
             rows = w[o * P * PACK : (o + 1) * P * PACK, cols]
-            nc.sync.dma_start(raw[:], rows.rearrange("(p j) c -> p j c", j=PACK))
+            nc.sync.dma_start(raw, rows.rearrange("(p j) c -> p j c", j=PACK))
             return raw
 
-        halves = [slice(0, HALF), slice(HALF, H)]
-        w1_raw = [[], []]
-        w3_raw = [[], []]
-        x_all = []
-        for o in range(PASSES):
-            w1_raw[0].append(load_rows("w1_raw0_%d" % o, w1, o, halves[0]))
-            if o == 0:
-                nc.sync.dma_start(offsets[:], offs)
-            if o == 1:
-                for q in range(4):
-                    nc.sync.dma_start(
-                        x_scale_rows[32 * q : 32 * q + 4 * PASSES, :].bitcast(I32),
-                        x_scales[:, 4 * q : 4 * q + 4, :].bitcast(I32),
-                    )
+        def load_x(o):
             words = sb("x_all%d" % o, [P, T], U32)
             nc.sync.dma_start(words[:].bitcast(I32), x_words[o].rearrange("p n t -> p (n t)").bitcast(I32))
-            x_all.append(words)
-        w3_raw[0] = [load_rows("w3_raw0_%d" % o, w3, o, halves[0]) for o in range(PASSES)]
-        w1_raw[1] = [load_rows("w1_raw1_%d" % o, w1, o, halves[1]) for o in range(PASSES)]
-        w3_raw[1] = [load_rows("w3_raw1_%d" % o, w3, o, halves[1]) for o in range(PASSES - 1)]
-        quarters = [slice(HALF, HALF + P), slice(HALF + P, H)]
-        w3_last = [load_rows("w3_last%d" % n, w3, PASSES - 1, quarters[n]) for n in range(2)]
-        w2_raw = load_rows("w2_raw", w2, 0, slice(0, N))
-        gate_sb = sb("gate_sb", [P, S], F32)
-        nc.sync.dma_start(gate_sb[:], gate[0:P, :])
+            return words
 
-        ident = sb("ident", [P, P], F32)
-        make_identity(nc, ident[:])
+        whole = slice(0, H)
+        w1_raw = [load_rows(raw_slot(0, [P, PACK, H])[:], w1, 0, whole)]
+        nc.sync.dma_start(offsets[:], offs)
+        x_all = [load_x(0), load_x(1)]
+        for q in range(4):
+            rows = slice(32 * q, 32 * q + 4 * PASSES)
+            nc.sync.dma_start(
+                x_scale_rows[rows, :].bitcast(I32),
+                x_scales[:, 4 * q : 4 * q + 4, :].bitcast(I32),
+            )
+        w1_raw.append(load_rows(raw_slot(1, [P, PACK, H])[:], w1, 1, whole))
+        x_all.append(load_x(2))
+        w1_raw.append(load_rows(raw_slot(2, [P, PACK, H])[:], w1, 2, whole))
         windows = []
         for m in range(N // P):
             window = sb("window%d" % m, [P, T], F32)
@@ -95,125 +80,139 @@ def tile_picked_depth_glu_relu_srt_p_kernel(
         x_codes = []
         x_planes = sb("x_planes", [P, S], U8)
 
-        def first_matmul(acc, g, o, codes, scales):
-            tokens = slice(g * P, (g + 1) * P)
-            nc.tensor.matmul_mx(
-                out=acc,
-                lhsT=x_codes[o][:, tokens].bitcast(FP8X4),
-                lhsT_scale=x_planes[4 * o : P, tokens],
-                rhs=codes.bitcast(FP8X4),
-                rhs_scale=scales,
-                start=(o == 0),
-                stop=(o == PASSES - 1),
-            )
+        def gather_words(o):
+            picked = keep.tile([P, S], U32, name="staging3" if o == 2 else "x_codes%d" % o, align_bytes=64)
+            nc.vector.tensor_copy(picked[:], x_all[o][:].indirect(offsets[:]))
+            x_codes.append(picked)
 
-        def cast_half(engine, grouped, raw, lo, hi):
-            dst = grouped.rearrange("p (c i j) -> p c j i", i=4, j=PACK)[:, lo:hi]
-            src = raw.rearrange("p j (c i) -> p c j i", i=4)[:, lo:hi]
-            cast(engine, dst, src)
+        def cast(engine, dst, src):
+            if engine == "scalar":
+                nc.scalar.copy(dst, src)
+            else:
+                nc.vector.tensor_copy(dst, src)
 
-        def prepare(name, raw, split):
-            width = raw.shape[2]
-            grouped = sb(name + "_bf", [P, width * PACK], BF16)
-            if split > 0:
-                cast_half("scalar", grouped[:], raw[:], 0, split)
-            if split < width // 4:
-                cast_half("vector", grouped[:], raw[:], split, width // 4)
-            codes = sb(name + "_codes", [P, width], U32)
-            scales = sb(name + "_scales", [P, width], U8)
-            quantise(codes[:], scales[:], grouped[:])
+        def staging(slot, shape):
+            return keep.tile(shape, BF16, name="staging%d" % slot, align_bytes=64)
+
+        def deal(codes, scales, raw, first, plan):
+            count = raw.shape[2] // PACK // len(plan)
+            src = raw.rearrange("p j (m t) -> p m j t", t=PACK)
+            for n, (engine, slot) in enumerate(plan):
+                grouped = staging(slot, [P, PACK, count, PACK])
+                cast(engine, grouped[:].rearrange("p t m j -> p m j t"), src[:, n * count : (n + 1) * count])
+                if count == P:
+                    quantise(
+                        codes[:].rearrange("p t m -> p (t m)"),
+                        scales[:].rearrange("p t m -> p (t m)"),
+                        grouped[:].rearrange("p t m j -> p (t m j)"),
+                    )
+                else:
+                    part = slice(first + n * count, first + (n + 1) * count)
+                    for t in range(PACK):
+                        quantise(codes[:, t, part], scales[:, t, part], grouped[:, t].rearrange("p m j -> p (m j)"))
+
+        def prepare(name, raw, plan):
+            codes = sb(name + "_codes", [P, PACK, P], U32)
+            scales = sb(name + "_scales", [P, PACK, P], U8)
+            deal(codes, scales, raw, 0, plan)
             return codes, scales
 
-        def gated(g, cols, a_rows, b_acc):
-            nc.vector.scalar_tensor_tensor(
-                out=h_rows[g][:, cols], in0=a_rows, scalar=0.0, in1=b_acc, op0=MAX, op1=MULT
-            )
-
-        W1_SPLIT = [[64, 64, 64], [64, 64, 32]]
-        W3_SPLIT = [[64, 0, 0], [32, 0]]
-        LAST_SPLIT = [0, 20]
-        h_rows = [sb("h_rows%d" % g, [P, H], BF16) for g in range(GROUPS)]
-
-        def first_product(hf):
-            a_acc = [bank(g, [P, HALF]) for g in range(GROUPS)]
-            for o in range(PASSES):
-                codes, scales = prepare("w1_%d_%d" % (hf, o), w1_raw[hf][o], W1_SPLIT[hf][o])
-                if hf == 0:
-                    picked = sb("x_codes%d" % o, [P, S], U32)
-                    nc.vector.tensor_copy(picked[:], x_all[o][:].indirect(offsets[:]))
-                    x_codes.append(picked)
-                    if o == 0:
-                        nc.vector.tensor_copy(x_planes[:], x_scale_rows[:].indirect(offsets[:]))
-                for g in range(GROUPS):
-                    first_matmul(a_acc[g][:], g, o, codes[:], scales[:])
-            return a_acc
-
-        def evacuate(a_acc, a_sb):
+        def first_pass(acc, o, codes, scales):
             for g in range(GROUPS):
-                nc.scalar.copy(a_sb[:, g, :], a_acc[g][:])
+                tokens = slice(g * P, (g + 1) * P)
+                for t in range(PACK):
+                    nc.tensor.matmul_mx(
+                        out=acc[g][:, t, :],
+                        lhsT=codes[:, t, :].bitcast(FP8X4),
+                        lhsT_scale=scales[:, t, :],
+                        rhs=x_codes[o][:, tokens].bitcast(FP8X4),
+                        rhs_scale=x_planes[4 * o : P, tokens],
+                        start=(o == 0 and t == 0),
+                        stop=(o == PASSES - 1 and t == PACK - 1),
+                    )
 
-        a_acc = first_product(0)
-        b_acc = [bank(GROUPS + g, [P, HALF]) for g in range(GROUPS)]
-        a_sb = w3_raw[0][0]
+        W1_PLAN = [[("scalar", 3)], [("scalar", 0)], [("vector", 0), ("scalar", 1)]]
+        W3_PLAN = [[("vector", 1), ("scalar", 2)], [("vector", 2), ("scalar", 0)]]
+        LAST_PLAN = [[("vector", 2), ("scalar", 1)], [("vector", 1), ("scalar", 0)]]
+
+        gather_words(0)
+        gather_words(1)
+        nc.vector.tensor_copy(x_planes[:], x_scale_rows[:].indirect(offsets[:]))
+        a_acc = [bank(g, [P, PACK, P]) for g in range(GROUPS)]
         for o in range(PASSES):
-            codes, scales = prepare("w3_0_%d" % o, w3_raw[0][o], W3_SPLIT[0][o])
+            codes, scales = prepare("w1_%d" % o, w1_raw[o], W1_PLAN[o])
             if o == 0:
-                evacuate(a_acc, a_sb)
-            for g in range(GROUPS):
-                first_matmul(b_acc[g][:], g, o, codes[:], scales[:])
-        for g in range(GROUPS):
-            gated(g, halves[0], a_sb[:, g, :], b_acc[g][:])
+                gather_words(2)
+            first_pass(a_acc, o, codes, scales)
 
-        a_acc = first_product(1)
-        a_sb = w3_raw[1][0]
-        early = []
-        for o in range(PASSES - 1):
-            early.append(prepare("w3_1_%d" % o, w3_raw[1][o], W3_SPLIT[1][o]))
-            if o == 0:
-                evacuate(a_acc, a_sb)
-        b_acc = []
+        w3_raw = [load_rows(raw_slot(o, [P, PACK, H])[:], w3, o, whole) for o in range(PASSES - 1)]
+        last_raw = raw_slot(2, [P, 2, PACK, H // 2])
+        w3_last = [load_rows(last_raw[:, n], w3, PASSES - 1, slice(n * H // 2, (n + 1) * H // 2)) for n in range(2)]
+
+        b_acc = [bank(GROUPS + g, [P, PACK, P]) for g in range(GROUPS)]
+        codes, scales = prepare("w3_0", w3_raw[0], W3_PLAN[0])
+        first_pass(b_acc, 0, codes, scales)
+
+        shared = raw_slot(0, [P, 2, PACK, N])
+        w2_raw = load_rows(shared[:, 1], w2, 0, slice(0, N))
+
+        def group_view(raw, first):
+            flat = raw.rearrange("p j c -> p (j c)")[:, first * P * PACK : (first + 1) * P * PACK]
+            return flat.rearrange("p (n t) -> p n t", t=PACK)
+
+        a_sb = [group_view(shared[:, 0], 0), group_view(shared[:, 0], 1), group_view(w2_raw, 0), group_view(w2_raw, 1)]
+
+        def evacuate(g):
+            nc.scalar.activation(a_sb[g], a_acc[g][:].rearrange("p t n -> p n t"), RELU)
+
+        evacuate(0)
+        evacuate(1)
+        codes, scales = prepare("w3_1", w3_raw[1], W3_PLAN[1])
+        first_pass(b_acc, 1, codes, scales)
+        gate_sb = raw_slot(1, [P, S])
+        nc.sync.dma_start(gate_sb[:], gate[0:P, :])
+        codes = sb("w3_last_codes", [P, PACK, P], U32)
+        scales = sb("w3_last_scales", [P, PACK, P], U8)
         for n in range(2):
-            b_acc.append([bank(GROUPS * (1 - n) + g, [P, P]) for g in range(GROUPS)])
-            cols = slice(n * P, (n + 1) * P)
-            for o in range(PASSES - 1):
-                for g in range(GROUPS):
-                    first_matmul(b_acc[n][g][:], g, o, early[o][0][:, cols], early[o][1][:, cols])
-        for n in range(2):
-            codes, scales = prepare("w3_last_%d" % n, w3_last[n], LAST_SPLIT[n])
-            for g in range(GROUPS):
-                first_matmul(b_acc[n][g][:], g, PASSES - 1, codes[:], scales[:])
+            deal(codes, scales, w3_last[n], n * P // 2, LAST_PLAN[n])
+        first_pass(b_acc, PASSES - 1, codes, scales)
 
         w2_codes = sb("w2_codes", [P, N], U32)
         w2_scales = sb("w2_scales", [P, N], U8)
-        w2_bf = sb("w2_bf", [P, N * PACK], BF16)
-        nc.scalar.copy(
-            w2_bf[:].rearrange("p (c i j) -> p c j i", i=4, j=PACK),
-            w2_raw[:].rearrange("p j (c i) -> p c j i", i=4),
-        )
-        quantise(w2_codes[:], w2_scales[:], w2_bf[:])
+        for m in (1, 0):
+            cols = slice(m * P, (m + 1) * P)
+            w2_bf = staging(1 + m, [P, P * PACK])
+            nc.scalar.copy(
+                w2_bf[:].rearrange("p (c i j) -> p c j i", i=4, j=PACK),
+                w2_raw[:, :, cols].rearrange("p j (c i) -> p c j i", i=4),
+            )
+            quantise(w2_codes[:, cols], w2_scales[:, cols], w2_bf[:])
+        evacuate(2)
+        evacuate(3)
 
-        y_sb = sb("y_sb", [P, N // P, S], F32)
+        y_gated = sb("y_gated", [P, N // P, S], F32)
+        y_rest = sb("y_rest", [P, S // 2], F32)
+
+        def entries(lo, hi):
+            return offsets[:, lo // LIST_COL : hi // LIST_COL]
+
+        def store_head(m):
+            head = sb("head%d" % m, [P, S // 2], F32)
+            nc.gpsimd.tensor_scalar(head[:], windows[m][:, 0 : S // 2], 1.0, 0.0, MULT, ADD)
+            nc.sync.dma_start(out[m * P : (m + 1) * P, 0 : S // 2], head[:])
+
         for g in range(GROUPS):
             tokens = slice(g * P, (g + 1) * P)
-            for n in range(2):
-                gated(g, quarters[n], a_sb[:, g, n * P : (n + 1) * P], b_acc[n][g][:])
-            turned = bank(GROUPS + g, [P, 2, P])
-            pairs = h_rows[g][:].bitcast(F32)
-            for u in range(2):
-                nc.tensor.transpose(turned[:, u, :], pairs[:, u : 2 * P : 2], ident[:])
-            grouped = sb("h_bf%d" % g, [P, P * PACK], BF16)
-            nc.scalar.copy(
-                grouped[:].bitcast(F32).rearrange("p (r u) -> p r u", u=2),
-                turned[:].rearrange("p u r -> p r u"),
-            )
+            grouped = staging(3 - g, [P, P, PACK]) if g in (1, 2) else sb("h_bf%d" % g, [P, P, PACK], BF16)
+            nc.vector.tensor_tensor(grouped[:], b_acc[g][:].rearrange("p t n -> p n t"), a_sb[g], MULT)
             codes = sb("h_codes%d" % g, [P, P], U32)
             scales = sb("h_scales%d" % g, [P, P], U8)
-            quantise(codes[:], scales[:], grouped[:])
-            y_acc = bank(g, [P, N // P, P])
-            for m in range(N // P):
+            quantise(codes[:], scales[:], grouped[:].rearrange("p n t -> p (n t)"))
+            y_acc = [bank(g, [P, P]), bank(GROUPS + g, [P, P])]
+            for m in (1, 0):
                 cols = slice(m * P, (m + 1) * P)
                 nc.tensor.matmul_mx(
-                    out=y_acc[:, m, :],
+                    out=y_acc[m][:],
                     lhsT=w2_codes[:, cols].bitcast(FP8X4),
                     lhsT_scale=w2_scales[:, cols],
                     rhs=codes[:].bitcast(FP8X4),
@@ -221,20 +220,16 @@ def tile_picked_depth_glu_relu_srt_p_kernel(
                     start=True,
                     stop=True,
                 )
-            nc.scalar.copy(y_sb[:, :, tokens], y_acc[:])
+            by_scalar = (1, 0) if g < 2 else (1,)
+            for m in by_scalar:
+                nc.vector.tensor_tensor(y_gated[:, m, tokens], y_acc[m][:], gate_sb[:, tokens], MULT)
+            if g >= 2:
+                cast("scalar" if g == 2 else "vector", y_rest[:, (g - 2) * P : (g - 1) * P], y_acc[0][:])
+            for m in by_scalar:
+                nc.scalar.activation(windows[m][:].indirect(entries(g * P, (g + 1) * P)), y_gated[:, m, tokens], COPY)
+                if g == 1:
+                    store_head(m)
 
-        def scatter(m, lo, hi):
-            nc.vector.tensor_tensor(
-                windows[m][:].indirect(offsets[:, lo // LIST_COL : hi // LIST_COL]),
-                y_sb[:, m, lo:hi],
-                gate_sb[:, lo:hi],
-                MULT,
-            )
-
-        for g in range(2):
-            scatter(0, g * P, (g + 1) * P)
-            scatter(1, g * P, (g + 1) * P)
-        scatter(0, S // 2, S)
-        nc.sync.dma_start(out[0:P, :], windows[0][:])
-        scatter(1, S // 2, S)
-        nc.sync.dma_start(out[P : 2 * P, :], windows[1][:])
+        nc.vector.tensor_tensor(windows[0][:].indirect(entries(S // 2, S)), y_rest[:], gate_sb[:, S // 2 : S], MULT)
+        nc.scalar.dma_start(out[P : 2 * P, S // 2 : T], windows[1][:, S // 2 : T])
+        nc.sync.dma_start(out[0:P, S // 2 : T], windows[0][:, S // 2 : T])

@@ -181,8 +181,9 @@ def tile_picked_depth_glu_relu_srt_p_kernel(
         w2_scales = sb("w2_scales", [P, N], U8)
         for m in (1, 0):
             cols = slice(m * P, (m + 1) * P)
-            w2_bf = staging(1 + m, [P, P * PACK])
-            nc.scalar.copy(
+            w2_bf = staging(2 * m, [P, P * PACK])
+            cast(
+                "scalar" if m == 1 else "vector",
                 w2_bf[:].rearrange("p (c i j) -> p c j i", i=4, j=PACK),
                 w2_raw[:, :, cols].rearrange("p j (c i) -> p c j i", i=4),
             )
@@ -191,7 +192,6 @@ def tile_picked_depth_glu_relu_srt_p_kernel(
         evacuate(3)
 
         y_gated = sb("y_gated", [P, N // P, S], F32)
-        y_rest = sb("y_rest", [P, S // 2], F32)
 
         def entries(lo, hi):
             return offsets[:, lo // LIST_COL : hi // LIST_COL]
@@ -203,7 +203,7 @@ def tile_picked_depth_glu_relu_srt_p_kernel(
 
         for g in range(GROUPS):
             tokens = slice(g * P, (g + 1) * P)
-            grouped = staging(3 - g, [P, P, PACK]) if g in (1, 2) else sb("h_bf%d" % g, [P, P, PACK], BF16)
+            grouped = staging(2, [P, P, PACK]) if g == 1 else sb("h_bf%d" % g, [P, P, PACK], BF16)
             nc.vector.tensor_tensor(grouped[:], b_acc[g][:].rearrange("p t n -> p n t"), a_sb[g], MULT)
             codes = sb("h_codes%d" % g, [P, P], U32)
             scales = sb("h_scales%d" % g, [P, P], U8)
@@ -220,16 +220,16 @@ def tile_picked_depth_glu_relu_srt_p_kernel(
                     start=True,
                     stop=True,
                 )
-            by_scalar = (1, 0) if g < 2 else (1,)
-            for m in by_scalar:
+            for m in (1, 0):
                 nc.vector.tensor_tensor(y_gated[:, m, tokens], y_acc[m][:], gate_sb[:, tokens], MULT)
-            if g >= 2:
-                cast("scalar" if g == 2 else "vector", y_rest[:, (g - 2) * P : (g - 1) * P], y_acc[0][:])
-            for m in by_scalar:
-                nc.scalar.activation(windows[m][:].indirect(entries(g * P, (g + 1) * P)), y_gated[:, m, tokens], COPY)
+            for m in (1, 0):
+                target = windows[m][:].indirect(entries(g * P, (g + 1) * P))
+                if g < GROUPS - 1:
+                    nc.scalar.activation(target, y_gated[:, m, tokens], COPY)
+                else:
+                    nc.vector.tensor_copy(target, y_gated[:, m, tokens])
                 if g == 1:
                     store_head(m)
 
-        nc.vector.tensor_tensor(windows[0][:].indirect(entries(S // 2, S)), y_rest[:], gate_sb[:, S // 2 : S], MULT)
-        nc.scalar.dma_start(out[P : 2 * P, S // 2 : T], windows[1][:, S // 2 : T])
-        nc.sync.dma_start(out[0:P, S // 2 : T], windows[0][:, S // 2 : T])
+        nc.sync.dma_start(out[P : 2 * P, S // 2 : T], windows[1][:, S // 2 : T])
+        nc.scalar.dma_start(out[0:P, S // 2 : T], windows[0][:, S // 2 : T])

@@ -43,7 +43,7 @@ def tile_picked_depth_glu_relu_srt_p_kernel(
 
         offsets = keep.tile([P, S // LIST_COL], U16, name="offsets")
         x_scale_rows = sb("x_scale_rows", [P, T], U8)
-        nc.gpsimd.memset(x_scale_rows[:].bitcast(I32), 0)
+        nc.vector.memset(x_scale_rows[:].bitcast(I32), 0)
 
         def raw_slot(slot, shape):
             return keep.tile(shape, F32, name="raw%d" % slot, align_bytes=64)
@@ -53,24 +53,18 @@ def tile_picked_depth_glu_relu_srt_p_kernel(
             nc.sync.dma_start(raw, rows.rearrange("(p j) c -> p j c", j=PACK))
             return raw
 
-        def load_x(o):
-            words = sb("x_all%d" % o, [P, T], U32)
-            nc.sync.dma_start(words[:].bitcast(I32), x_words[o].rearrange("p n t -> p (n t)").bitcast(I32))
-            return words
-
         whole = slice(0, H)
-        w1_raw = [load_rows(raw_slot(0, [P, PACK, H])[:], w1, 0, whole)]
+        x_all = sb("x_all", [P, PASSES, T], U32)
+        nc.sync.dma_start(x_all[:].bitcast(I32), x_words.rearrange("o p n t -> p o (n t)").bitcast(I32))
         nc.sync.dma_start(offsets[:], offs)
-        x_all = [load_x(0), load_x(1)]
+        w1_raw = [load_rows(raw_slot(0, [P, PACK, H])[:], w1, 0, whole)]
         for q in range(4):
             rows = slice(32 * q, 32 * q + 4 * PASSES)
             nc.sync.dma_start(
                 x_scale_rows[rows, :].bitcast(I32),
                 x_scales[:, 4 * q : 4 * q + 4, :].bitcast(I32),
             )
-        w1_raw.append(load_rows(raw_slot(1, [P, PACK, H])[:], w1, 1, whole))
-        x_all.append(load_x(2))
-        w1_raw.append(load_rows(raw_slot(2, [P, PACK, H])[:], w1, 2, whole))
+        w1_raw.extend([load_rows(raw_slot(o, [P, PACK, H])[:], w1, o, whole) for o in range(1, PASSES)])
         windows = []
         for m in range(N // P):
             window = sb("window%d" % m, [P, T], F32)
@@ -81,8 +75,8 @@ def tile_picked_depth_glu_relu_srt_p_kernel(
         x_planes = sb("x_planes", [P, S], U8)
 
         def gather_words(o):
-            picked = keep.tile([P, S], U32, name="staging3" if o == 2 else "x_codes%d" % o, align_bytes=64)
-            nc.vector.tensor_copy(picked[:], x_all[o][:].indirect(offsets[:]))
+            picked = sb("x_codes%d" % o, [P, S], U32)
+            nc.vector.tensor_copy(picked[:], x_all[:, o, :].indirect(offsets[:]))
             x_codes.append(picked)
 
         def cast(engine, dst, src):
@@ -131,18 +125,17 @@ def tile_picked_depth_glu_relu_srt_p_kernel(
                         stop=(o == PASSES - 1 and t == PACK - 1),
                     )
 
-        W1_PLAN = [[("scalar", 3)], [("scalar", 0)], [("vector", 0), ("scalar", 1)]]
-        W3_PLAN = [[("vector", 1), ("scalar", 2)], [("vector", 2), ("scalar", 0)]]
-        LAST_PLAN = [[("vector", 2), ("scalar", 1)], [("vector", 1), ("scalar", 0)]]
+        W1_PLAN = [[("scalar", 0)], [("vector", 0), ("scalar", 1)], [("vector", 1), ("scalar", 2)]]
+        W3_PLAN = [[("vector", 2), ("scalar", 0)], [("vector", 0), ("scalar", 1)]]
+        LAST_PLAN = [[("vector", 0), ("scalar", 2)], [("vector", 2), ("scalar", 1)]]
 
         gather_words(0)
         gather_words(1)
+        gather_words(2)
         nc.vector.tensor_copy(x_planes[:], x_scale_rows[:].indirect(offsets[:]))
         a_acc = [bank(g, [P, PACK, P]) for g in range(GROUPS)]
         for o in range(PASSES):
             codes, scales = prepare("w1_%d" % o, w1_raw[o], W1_PLAN[o])
-            if o == 0:
-                gather_words(2)
             first_pass(a_acc, o, codes, scales)
 
         w3_raw = [load_rows(raw_slot(o, [P, PACK, H])[:], w3, o, whole) for o in range(PASSES - 1)]
@@ -181,7 +174,7 @@ def tile_picked_depth_glu_relu_srt_p_kernel(
         w2_scales = sb("w2_scales", [P, N], U8)
         for m in (1, 0):
             cols = slice(m * P, (m + 1) * P)
-            w2_bf = staging(2 * m, [P, P * PACK])
+            w2_bf = staging(1 - m, [P, P * PACK])
             cast(
                 "scalar" if m == 1 else "vector",
                 w2_bf[:].rearrange("p (c i j) -> p c j i", i=4, j=PACK),
@@ -203,7 +196,7 @@ def tile_picked_depth_glu_relu_srt_p_kernel(
 
         for g in range(GROUPS):
             tokens = slice(g * P, (g + 1) * P)
-            grouped = staging(2, [P, P, PACK]) if g == 1 else sb("h_bf%d" % g, [P, P, PACK], BF16)
+            grouped = staging(0, [P, P, PACK]) if g == 1 else sb("h_bf%d" % g, [P, P, PACK], BF16)
             nc.vector.tensor_tensor(grouped[:], b_acc[g][:].rearrange("p t n -> p n t"), a_sb[g], MULT)
             codes = sb("h_codes%d" % g, [P, P], U32)
             scales = sb("h_scales%d" % g, [P, P], U8)

@@ -13,7 +13,6 @@ U16 = mybir.dt.uint16
 U8 = mybir.dt.uint8
 FP8X4 = mybir.dt.float8_e4m3fn_x4
 MULT = mybir.AluOpType.mult
-ADD = mybir.AluOpType.add
 RELU = mybir.ActivationFunctionType.Relu
 COPY = mybir.ActivationFunctionType.Copy
 
@@ -189,10 +188,17 @@ def tile_picked_depth_glu_relu_srt_p_kernel(
         def entries(lo, hi):
             return offsets[:, lo // LIST_COL : hi // LIST_COL]
 
-        def store_head(m):
-            head = sb("head%d" % m, [P, S // 2], F32)
-            nc.gpsimd.tensor_scalar(head[:], windows[m][:, 0 : S // 2], 1.0, 0.0, MULT, ADD)
-            nc.sync.dma_start(out[m * P : (m + 1) * P, 0 : S // 2], head[:])
+        def store_head(m, head):
+            nc.vector.tensor_copy(head, windows[m][:, 0 : S // 2])
+            nc.sync.dma_start(out[m * P : (m + 1) * P, 0 : S // 2], head)
+
+        def scatter(g):
+            for m in (1, 0):
+                target = windows[m][:].indirect(entries(g * P, (g + 1) * P))
+                if g < GROUPS - 1:
+                    nc.scalar.activation(target, y_gated[:, m, g * P : (g + 1) * P], COPY)
+                else:
+                    nc.vector.tensor_copy(target, y_gated[:, m, g * P : (g + 1) * P])
 
         for g in range(GROUPS):
             tokens = slice(g * P, (g + 1) * P)
@@ -215,14 +221,12 @@ def tile_picked_depth_glu_relu_srt_p_kernel(
                 )
             for m in (1, 0):
                 nc.vector.tensor_tensor(y_gated[:, m, tokens], y_acc[m][:], gate_sb[:, tokens], MULT)
-            for m in (1, 0):
-                target = windows[m][:].indirect(entries(g * P, (g + 1) * P))
-                if g < GROUPS - 1:
-                    nc.scalar.activation(target, y_gated[:, m, tokens], COPY)
-                else:
-                    nc.vector.tensor_copy(target, y_gated[:, m, tokens])
-                if g == 1:
-                    store_head(m)
+            if g < 2:
+                scatter(g)
 
+        store_head(1, a_sb[GROUPS - 1].rearrange("p n t -> p (n t)")[:, 0 : S // 2])
+        store_head(0, sb("h_bf%d" % (GROUPS - 1), [P, S // 2], F32)[:])
+        scatter(2)
+        scatter(3)
         nc.sync.dma_start(out[P : 2 * P, S // 2 : T], windows[1][:, S // 2 : T])
         nc.scalar.dma_start(out[0:P, S // 2 : T], windows[0][:, S // 2 : T])

@@ -53,7 +53,7 @@ def tile_picked_depth_glu_relu_srt_p_kernel(
             return raw
 
         whole = slice(0, H)
-        x_all = sb("x_all", [P, PASSES, T], U32)
+        x_all = sb("raw3", [P, PASSES, T], U32)
         nc.sync.dma_start(x_all[:].bitcast(I32), x_words.rearrange("o p n t -> p o (n t)").bitcast(I32))
         nc.sync.dma_start(offsets[:], offs)
         w1_raw = [load_rows(raw_slot(0, [P, PACK, H])[:], w1, 0, whole)]
@@ -137,15 +137,15 @@ def tile_picked_depth_glu_relu_srt_p_kernel(
             codes, scales = prepare("w1_%d" % o, w1_raw[o], W1_PLAN[o])
             first_pass(a_acc, o, codes, scales)
 
-        w3_raw = [load_rows(raw_slot(o, [P, PACK, H])[:], w3, o, whole) for o in range(PASSES - 1)]
-        last_raw = raw_slot(2, [P, 2, PACK, H // 2])
+        w3_raw = [load_rows(raw_slot((3, 0)[o], [P, PACK, H])[:], w3, o, whole) for o in range(PASSES - 1)]
+        last_raw = raw_slot(1, [P, 2, PACK, H // 2])
         w3_last = [load_rows(last_raw[:, n], w3, PASSES - 1, slice(n * H // 2, (n + 1) * H // 2)) for n in range(2)]
 
         b_acc = [bank(GROUPS + g, [P, PACK, P]) for g in range(GROUPS)]
         codes, scales = prepare("w3_0", w3_raw[0], W3_PLAN[0])
         first_pass(b_acc, 0, codes, scales)
 
-        shared = raw_slot(0, [P, 2, PACK, N])
+        shared = raw_slot(3, [P, 2, PACK, N])
         w2_raw = load_rows(shared[:, 1], w2, 0, slice(0, N))
 
         def group_view(raw, first):
@@ -161,7 +161,7 @@ def tile_picked_depth_glu_relu_srt_p_kernel(
         evacuate(1)
         codes, scales = prepare("w3_1", w3_raw[1], W3_PLAN[1])
         first_pass(b_acc, 1, codes, scales)
-        gate_sb = raw_slot(1, [P, S])
+        gate_sb = raw_slot(0, [P, S])
         nc.sync.dma_start(gate_sb[:], gate[0:P, :])
         codes = sb("w3_last_codes", [P, PACK, P], U32)
         scales = sb("w3_last_scales", [P, PACK, P], U8)

@@ -21,6 +21,7 @@ PACK = 4
 PASSES = K // (P * PACK)
 GROUPS = S // P
 LIST_COL = 16
+HEAD = S // 2
 
 
 def tile_picked_depth_glu_relu_srt_p_kernel(
@@ -40,30 +41,45 @@ def tile_picked_depth_glu_relu_srt_p_kernel(
         def quantise(codes, scales, grouped):
             nc.vector.quantize_mx(out=codes.bitcast(FP8X4), scales=scales, in_=grouped)
 
+        def cast(engine, dst, src):
+            if engine == "scalar":
+                nc.scalar.copy(dst, src)
+            else:
+                nc.vector.tensor_copy(dst, src)
+
         offsets = keep.tile([P, S // LIST_COL], U16, name="offsets")
         x_scale_rows = sb("x_scale_rows", [P, T], U8)
         nc.vector.memset(x_scale_rows[:].bitcast(I32), 0)
 
-        def raw_slot(slot, shape):
-            return keep.tile(shape, F32, name="raw%d" % slot, align_bytes=64)
-
-        def load_rows(raw, w, o, cols):
+        def load_rows(name, w, o, cols):
+            raw = sb(name, [P, PACK, cols.stop - cols.start], F32)
             rows = w[o * P * PACK : (o + 1) * P * PACK, cols]
-            nc.sync.dma_start(raw, rows.rearrange("(p j) c -> p j c", j=PACK))
+            nc.sync.dma_start(raw[:], rows.rearrange("(p j) c -> p j c", j=PACK))
             return raw
 
         whole = slice(0, H)
-        x_all = sb("raw3", [P, PASSES, T], U32)
+        x_all = sb("x_all", [P, PASSES, T], U32)
         nc.sync.dma_start(x_all[:].bitcast(I32), x_words.rearrange("o p n t -> p o (n t)").bitcast(I32))
         nc.sync.dma_start(offsets[:], offs)
-        w1_raw = [load_rows(raw_slot(0, [P, PACK, H])[:], w1, 0, whole)]
+        w1_raw = [load_rows("w1_raw0", w1, 0, whole)]
         for q in range(4):
             rows = slice(32 * q, 32 * q + 4 * PASSES)
             nc.sync.dma_start(
                 x_scale_rows[rows, :].bitcast(I32),
                 x_scales[:, 4 * q : 4 * q + 4, :].bitcast(I32),
             )
-        w1_raw.extend([load_rows(raw_slot(o, [P, PACK, H])[:], w1, o, whole) for o in range(1, PASSES)])
+        w1_raw.extend([load_rows("w1_raw%d" % o, w1, o, whole) for o in range(1, PASSES)])
+        w3_raw = [load_rows("w3_raw%d" % o, w3, o, whole) for o in range(PASSES - 1)]
+        w3_last = [
+            load_rows("w3_last%d" % n, w3, PASSES - 1, slice(n * H // 2, (n + 1) * H // 2)) for n in range(2)
+        ]
+        w2_raw = load_rows("w2_raw", w2, 0, slice(0, N))
+        gate_sb = []
+        for n, tokens in enumerate((slice(0, P), slice(P, S))):
+            piece = sb("gate%d" % n, [P, tokens.stop - tokens.start], F32)
+            nc.sync.dma_start(piece[:], gate[0:P, tokens])
+            gate_sb.extend([piece[:, c : c + P] for c in range(0, tokens.stop - tokens.start, P)])
+
         windows = []
         for m in range(N // P):
             window = sb("window%d" % m, [P, T], F32)
@@ -71,47 +87,39 @@ def tile_picked_depth_glu_relu_srt_p_kernel(
             windows.append(window)
 
         x_codes = []
-        x_planes = sb("x_planes", [P, S], U8)
-
-        def gather_words(o):
+        for o in range(PASSES):
             picked = sb("x_codes%d" % o, [P, S], U32)
             nc.vector.tensor_copy(picked[:], x_all[:, o, :].indirect(offsets[:]))
             x_codes.append(picked)
+        x_planes = sb("x_planes", [P, S], U8)
+        nc.vector.tensor_copy(x_planes[:], x_scale_rows[:].indirect(offsets[:]))
 
-        def cast(engine, dst, src):
-            if engine == "scalar":
-                nc.scalar.copy(dst, src)
-            else:
-                nc.vector.tensor_copy(dst, src)
-
-        def staging(slot, shape):
-            return keep.tile(shape, BF16, name="staging%d" % slot, align_bytes=64)
-
-        def deal(codes, scales, raw, first, plan):
-            count = raw.shape[2] // PACK // len(plan)
-            src = raw.rearrange("p j (m t) -> p m j t", t=PACK)
-            for n, (engine, slot) in enumerate(plan):
-                grouped = staging(slot, [P, PACK, count, PACK])
-                cast(engine, grouped[:].rearrange("p t m j -> p m j t"), src[:, n * count : (n + 1) * count])
+        def deal(name, codes, scales, raw, first, plan):
+            src = raw[:].rearrange("p j (m t) -> p m j t", t=PACK)
+            for n, (engine, ts, ms) in enumerate(plan):
+                count = ms.stop - ms.start
+                grouped = sb("%s_bf%d" % (name, n), [P, ts.stop - ts.start, count, PACK], BF16)
+                cast(engine, grouped[:].rearrange("p t m j -> p m j t"), src[:, ms, :, ts])
                 if count == P:
                     quantise(
-                        codes[:].rearrange("p t m -> p (t m)"),
-                        scales[:].rearrange("p t m -> p (t m)"),
+                        codes[:, ts, :].rearrange("p t m -> p (t m)"),
+                        scales[:, ts, :].rearrange("p t m -> p (t m)"),
                         grouped[:].rearrange("p t m j -> p (t m j)"),
                     )
                 else:
-                    part = slice(first + n * count, first + (n + 1) * count)
-                    for t in range(PACK):
-                        quantise(codes[:, t, part], scales[:, t, part], grouped[:, t].rearrange("p m j -> p (m j)"))
+                    part = slice(first + ms.start, first + ms.stop)
+                    for t in range(ts.start, ts.stop):
+                        quantise(
+                            codes[:, t, part],
+                            scales[:, t, part],
+                            grouped[:, t - ts.start].rearrange("p m j -> p (m j)"),
+                        )
 
-        def prepare(name, raw, plan):
-            codes = sb(name + "_codes", [P, PACK, P], U32)
-            scales = sb(name + "_scales", [P, PACK, P], U8)
-            deal(codes, scales, raw, 0, plan)
-            return codes, scales
+        def code_tiles(name):
+            return sb(name + "_codes", [P, PACK, P], U32), sb(name + "_scales", [P, PACK, P], U8)
 
-        def first_pass(acc, o, codes, scales):
-            for g in range(GROUPS):
+        def first_pass(acc, o, codes, scales, order):
+            for g in order:
                 tokens = slice(g * P, (g + 1) * P)
                 for t in range(PACK):
                     nc.tensor.matmul_mx(
@@ -124,109 +132,129 @@ def tile_picked_depth_glu_relu_srt_p_kernel(
                         stop=(o == PASSES - 1 and t == PACK - 1),
                     )
 
-        W1_PLAN = [[("scalar", 0)], [("vector", 0), ("scalar", 1)], [("vector", 1), ("scalar", 2)]]
-        W3_PLAN = [[("vector", 2), ("scalar", 0)], [("vector", 0), ("scalar", 1)]]
-        LAST_PLAN = [[("vector", 0), ("scalar", 2)], [("vector", 2), ("scalar", 1)]]
+        low, high, every_t = slice(0, 2), slice(2, 4), slice(0, 4)
+        every_m, half_m, other_m = slice(0, P), slice(0, P // 2), slice(P // 2, P)
+        all_scalar = [("scalar", every_t, every_m)]
+        halves = [("vector", low, every_m), ("scalar", high, every_m)]
+        quarter = [("vector", low, every_m), ("vector", high, half_m), ("scalar", high, other_m)]
+        last_halves = [("vector", low, half_m), ("scalar", high, half_m)]
+        order = (0, 3, 1, 2)
 
-        gather_words(0)
-        gather_words(1)
-        gather_words(2)
-        nc.vector.tensor_copy(x_planes[:], x_scale_rows[:].indirect(offsets[:]))
         a_acc = [bank(g, [P, PACK, P]) for g in range(GROUPS)]
-        for o in range(PASSES):
-            codes, scales = prepare("w1_%d" % o, w1_raw[o], W1_PLAN[o])
-            first_pass(a_acc, o, codes, scales)
-
-        w3_raw = [load_rows(raw_slot((3, 0)[o], [P, PACK, H])[:], w3, o, whole) for o in range(PASSES - 1)]
-        last_raw = raw_slot(1, [P, 2, PACK, H // 2])
-        w3_last = [load_rows(last_raw[:, n], w3, PASSES - 1, slice(n * H // 2, (n + 1) * H // 2)) for n in range(2)]
+        for o, plan in enumerate((all_scalar, halves, halves)):
+            codes, scales = code_tiles("w1_%d" % o)
+            deal("w1_%d" % o, codes, scales, w1_raw[o], 0, plan)
+            first_pass(a_acc, o, codes, scales, order)
 
         b_acc = [bank(GROUPS + g, [P, PACK, P]) for g in range(GROUPS)]
-        codes, scales = prepare("w3_0", w3_raw[0], W3_PLAN[0])
-        first_pass(b_acc, 0, codes, scales)
+        codes, scales = code_tiles("w3_0")
+        deal("w3_0", codes, scales, w3_raw[0], 0, quarter)
+        first_pass(b_acc, 0, codes, scales, order)
 
-        shared = raw_slot(3, [P, 2, PACK, N])
-        w2_raw = load_rows(shared[:, 1], w2, 0, slice(0, N))
+        def interleaved(acc):
+            return acc[:].rearrange("p t n -> p n t")
 
-        def group_view(raw, first):
-            flat = raw.rearrange("p j c -> p (j c)")[:, first * P * PACK : (first + 1) * P * PACK]
-            return flat.rearrange("p (n t) -> p n t", t=PACK)
+        a_early = sb("w3_raw0", [P, 3, P, PACK], F32)
+        a_sb = {0: a_early[:, 0], 3: a_early[:, 1], 1: a_early[:, 2]}
+        for g in order[:3]:
+            nc.scalar.activation(a_sb[g], interleaved(a_acc[g]), RELU)
 
-        a_sb = [group_view(shared[:, 0], 0), group_view(shared[:, 0], 1), group_view(w2_raw, 0), group_view(w2_raw, 1)]
-
-        def evacuate(g):
-            nc.scalar.activation(a_sb[g], a_acc[g][:].rearrange("p t n -> p n t"), RELU)
-
-        evacuate(0)
-        evacuate(1)
-        codes, scales = prepare("w3_1", w3_raw[1], W3_PLAN[1])
-        first_pass(b_acc, 1, codes, scales)
-        gate_sb = raw_slot(0, [P, S])
-        nc.sync.dma_start(gate_sb[:], gate[0:P, :])
-        codes = sb("w3_last_codes", [P, PACK, P], U32)
-        scales = sb("w3_last_scales", [P, PACK, P], U8)
+        codes, scales = code_tiles("w3_1")
+        deal("w3_1", codes, scales, w3_raw[1], 0, halves)
+        first_pass(b_acc, 1, codes, scales, order)
+        codes, scales = code_tiles("w3_2")
         for n in range(2):
-            deal(codes, scales, w3_last[n], n * P // 2, LAST_PLAN[n])
-        first_pass(b_acc, PASSES - 1, codes, scales)
+            deal("w3_last%d" % n, codes, scales, w3_last[n], n * P // 2, last_halves)
+        first_pass(b_acc, PASSES - 1, codes, scales, order)
+
+        a_sb[2] = sb("w3_last1", [P, P, PACK], F32)[:]
+        nc.scalar.activation(a_sb[2], interleaved(a_acc[2]), RELU)
 
         w2_codes = sb("w2_codes", [P, N], U32)
         w2_scales = sb("w2_scales", [P, N], U8)
         for m in (1, 0):
             cols = slice(m * P, (m + 1) * P)
-            w2_bf = staging(1 - m, [P, P * PACK])
+            w2_bf = sb("w2_bf%d" % m, [P, P * PACK], BF16)
             cast(
                 "scalar" if m == 1 else "vector",
                 w2_bf[:].rearrange("p (c i j) -> p c j i", i=4, j=PACK),
                 w2_raw[:, :, cols].rearrange("p j (c i) -> p c j i", i=4),
             )
             quantise(w2_codes[:, cols], w2_scales[:, cols], w2_bf[:])
-        evacuate(2)
-        evacuate(3)
+
+        b_last = []
+        for n in range(2):
+            half = sb("b_last%d" % n, [P, P // 2, PACK], F32)
+            nc.scalar.copy(half[:], interleaved(b_acc[3])[:, n * P // 2 : (n + 1) * P // 2])
+            b_last.append(half)
 
         y_gated = sb("y_gated", [P, N // P, S], F32)
 
         def entries(lo, hi):
             return offsets[:, lo // LIST_COL : hi // LIST_COL]
 
-        def store_head(m, head):
-            nc.vector.tensor_copy(head, windows[m][:, 0 : S // 2])
-            nc.sync.dma_start(out[m * P : (m + 1) * P, 0 : S // 2], head)
+        def product(g, slot):
+            grouped = sb(slot, [P, P, PACK], BF16)
+            nc.vector.tensor_tensor(grouped[:], interleaved(b_acc[g]), a_sb[g], MULT)
+            return grouped[:].rearrange("p n t -> p (n t)")
 
-        def scatter(g):
-            for m in (1, 0):
-                target = windows[m][:].indirect(entries(g * P, (g + 1) * P))
-                if g < GROUPS - 1:
-                    nc.scalar.activation(target, y_gated[:, m, g * P : (g + 1) * P], COPY)
-                else:
-                    nc.vector.tensor_copy(target, y_gated[:, m, g * P : (g + 1) * P])
+        def side_product(n, slot):
+            tokens = slice(n * P // 2, (n + 1) * P // 2)
+            grouped = sb(slot, [P, P // 2, PACK], BF16)
+            nc.gpsimd.tensor_tensor(grouped[:], b_last[n][:], a_sb[3][:, tokens], MULT)
+            return grouped[:].rearrange("p n t -> p (n t)")
 
-        for g in range(GROUPS):
-            tokens = slice(g * P, (g + 1) * P)
-            grouped = staging(0, [P, P, PACK]) if g == 1 else sb("h_bf%d" % g, [P, P, PACK], BF16)
-            nc.vector.tensor_tensor(grouped[:], b_acc[g][:].rearrange("p t n -> p n t"), a_sb[g], MULT)
+        def second(g, m, codes, scales):
+            cols = slice(m * P, (m + 1) * P)
+            y_acc = bank(g if m == 1 else GROUPS + g, [P, P])
+            nc.tensor.matmul_mx(
+                out=y_acc[:],
+                lhsT=w2_codes[:, cols].bitcast(FP8X4),
+                lhsT_scale=w2_scales[:, cols],
+                rhs=codes.bitcast(FP8X4),
+                rhs_scale=scales,
+                start=True,
+                stop=True,
+            )
+            return y_acc
+
+        def gated(g, m, y_acc):
+            nc.vector.tensor_tensor(y_gated[:, m, g * P : (g + 1) * P], y_acc[:], gate_sb[g], MULT)
+
+        def early_group(g, slot):
+            h = product(g, slot)
             codes = sb("h_codes%d" % g, [P, P], U32)
             scales = sb("h_scales%d" % g, [P, P], U8)
-            quantise(codes[:], scales[:], grouped[:].rearrange("p n t -> p (n t)"))
-            y_acc = [bank(g, [P, P]), bank(GROUPS + g, [P, P])]
+            quantise(codes[:], scales[:], h)
+            ys = [second(g, m, codes[:], scales[:]) for m in (1, 0)]
+            for m, y_acc in zip((1, 0), ys):
+                gated(g, m, y_acc)
             for m in (1, 0):
-                cols = slice(m * P, (m + 1) * P)
-                nc.tensor.matmul_mx(
-                    out=y_acc[m][:],
-                    lhsT=w2_codes[:, cols].bitcast(FP8X4),
-                    lhsT_scale=w2_scales[:, cols],
-                    rhs=codes[:].bitcast(FP8X4),
-                    rhs_scale=scales[:],
-                    start=True,
-                    stop=True,
-                )
-            for m in (1, 0):
-                nc.vector.tensor_tensor(y_gated[:, m, tokens], y_acc[m][:], gate_sb[:, tokens], MULT)
-            if g < 2:
-                scatter(g)
+                target = windows[m][:].indirect(entries(g * P, (g + 1) * P))
+                nc.scalar.activation(target, y_gated[:, m, g * P : (g + 1) * P], COPY)
 
-        store_head(1, a_sb[GROUPS - 1].rearrange("p n t -> p (n t)")[:, 0 : S // 2])
-        store_head(0, sb("h_bf%d" % (GROUPS - 1), [P, S // 2], F32)[:])
-        scatter(2)
-        scatter(3)
-        nc.sync.dma_start(out[P : 2 * P, S // 2 : T], windows[1][:, S // 2 : T])
-        nc.scalar.dma_start(out[0:P, S // 2 : T], windows[0][:, S // 2 : T])
+        early_group(0, "h_bf0")
+        h3 = [side_product(0, "h_bf0")]
+        early_group(1, "w2_bf0")
+        h3.append(side_product(1, "w2_bf0"))
+        h2 = product(2, "gate0")
+        codes = sb("b_last1", [P, 2 * P], U32)
+        scales = sb("h_scales23", [P, 2 * P], U8)
+        quantise(codes[:, 0:P], scales[:, 0:P], h2)
+        for n in range(2):
+            part = slice(P + n * P // 2, P + (n + 1) * P // 2)
+            quantise(codes[:, part], scales[:, part], h3[n])
+        for m in (1, 0):
+            head = sb("head%d" % m, [P, HEAD], F32)
+            nc.gpsimd.tensor_copy(head[:], windows[m][:, 0:HEAD])
+            nc.sync.dma_start(out[m * P : (m + 1) * P, 0:HEAD], head[:])
+        for m in (1, 0):
+            for g in (2, 3):
+                part = slice((g - 2) * P, (g - 1) * P)
+                gated(g, m, second(g, m, codes[:, part], scales[:, part]))
+        for g in (2, 3):
+            target = windows[1][:].indirect(entries(g * P, (g + 1) * P))
+            nc.scalar.activation(target, y_gated[:, 1, g * P : (g + 1) * P], COPY)
+        nc.vector.tensor_copy(windows[0][:].indirect(entries(HEAD, S)), y_gated[:, 0, HEAD:S])
+        nc.scalar.dma_start(out[P : 2 * P, HEAD:T], windows[1][:, HEAD:T])
+        nc.sync.dma_start(out[0:P, HEAD:T], windows[0][:, HEAD:T])

@@ -74,11 +74,8 @@ def tile_picked_depth_glu_relu_srt_p_kernel(
             load_rows("w3_last%d" % n, w3, PASSES - 1, slice(n * H // 2, (n + 1) * H // 2)) for n in range(2)
         ]
         w2_raw = load_rows("w2_raw", w2, 0, slice(0, N))
-        gate_sb = []
-        for n, tokens in enumerate((slice(0, P), slice(P, S))):
-            piece = sb("gate%d" % n, [P, tokens.stop - tokens.start], F32)
-            nc.sync.dma_start(piece[:], gate[0:P, tokens])
-            gate_sb.extend([piece[:, c : c + P] for c in range(0, tokens.stop - tokens.start, P)])
+        gate_sb = sb("gate_sb", [P, S], F32)
+        nc.sync.dma_start(gate_sb[:], gate[0:P, :])
 
         windows = []
         for m in range(N // P):
@@ -138,7 +135,7 @@ def tile_picked_depth_glu_relu_srt_p_kernel(
         halves = [("vector", low, every_m), ("scalar", high, every_m)]
         quarter = [("vector", low, every_m), ("vector", high, half_m), ("scalar", high, other_m)]
         last_halves = [("vector", low, half_m), ("scalar", high, half_m)]
-        order = (0, 3, 1, 2)
+        order = range(GROUPS)
 
         a_acc = [bank(g, [P, PACK, P]) for g in range(GROUPS)]
         for o, plan in enumerate((all_scalar, halves, halves)):
@@ -155,8 +152,8 @@ def tile_picked_depth_glu_relu_srt_p_kernel(
             return acc[:].rearrange("p t n -> p n t")
 
         a_early = sb("w3_raw0", [P, 3, P, PACK], F32)
-        a_sb = {0: a_early[:, 0], 3: a_early[:, 1], 1: a_early[:, 2]}
-        for g in order[:3]:
+        a_sb = [a_early[:, g] for g in range(GROUPS - 1)]
+        for g in range(GROUPS - 1):
             nc.scalar.activation(a_sb[g], interleaved(a_acc[g]), RELU)
 
         codes, scales = code_tiles("w3_1")
@@ -167,8 +164,8 @@ def tile_picked_depth_glu_relu_srt_p_kernel(
             deal("w3_last%d" % n, codes, scales, w3_last[n], n * P // 2, last_halves)
         first_pass(b_acc, PASSES - 1, codes, scales, order)
 
-        a_sb[2] = sb("w3_last1", [P, P, PACK], F32)[:]
-        nc.scalar.activation(a_sb[2], interleaved(a_acc[2]), RELU)
+        a_sb.append(sb("w3_last1", [P, P, PACK], F32)[:])
+        nc.scalar.activation(a_sb[3], interleaved(a_acc[3]), RELU)
 
         w2_codes = sb("w2_codes", [P, N], U32)
         w2_scales = sb("w2_scales", [P, N], U8)
@@ -182,13 +179,11 @@ def tile_picked_depth_glu_relu_srt_p_kernel(
             )
             quantise(w2_codes[:, cols], w2_scales[:, cols], w2_bf[:])
 
-        b_last = []
-        for n in range(2):
-            half = sb("b_last%d" % n, [P, P // 2, PACK], F32)
-            nc.scalar.copy(half[:], interleaved(b_acc[3])[:, n * P // 2 : (n + 1) * P // 2])
-            b_last.append(half)
+        y_gated = [sb("y_gated%d" % m, [P, 3 * P], F32) for m in range(N // P)]
 
-        y_gated = sb("y_gated", [P, N // P, S], F32)
+        def place(g, count=1):
+            first = (0, 2, 1, 2)[g] * P
+            return slice(first, first + count * P)
 
         def entries(lo, hi):
             return offsets[:, lo // LIST_COL : hi // LIST_COL]
@@ -196,12 +191,6 @@ def tile_picked_depth_glu_relu_srt_p_kernel(
         def product(g, slot):
             grouped = sb(slot, [P, P, PACK], BF16)
             nc.vector.tensor_tensor(grouped[:], interleaved(b_acc[g]), a_sb[g], MULT)
-            return grouped[:].rearrange("p n t -> p (n t)")
-
-        def side_product(n, slot):
-            tokens = slice(n * P // 2, (n + 1) * P // 2)
-            grouped = sb(slot, [P, P // 2, PACK], BF16)
-            nc.gpsimd.tensor_tensor(grouped[:], b_last[n][:], a_sb[3][:, tokens], MULT)
             return grouped[:].rearrange("p n t -> p (n t)")
 
         def second(g, m, codes, scales):
@@ -219,42 +208,42 @@ def tile_picked_depth_glu_relu_srt_p_kernel(
             return y_acc
 
         def gated(g, m, y_acc):
-            nc.vector.tensor_tensor(y_gated[:, m, g * P : (g + 1) * P], y_acc[:], gate_sb[g], MULT)
+            nc.vector.tensor_tensor(y_gated[m][:, place(g)], y_acc[:], gate_sb[:, g * P : (g + 1) * P], MULT)
 
-        def early_group(g, slot):
-            h = product(g, slot)
+        def second_product(g, h):
             codes = sb("h_codes%d" % g, [P, P], U32)
             scales = sb("h_scales%d" % g, [P, P], U8)
             quantise(codes[:], scales[:], h)
-            ys = [second(g, m, codes[:], scales[:]) for m in (1, 0)]
-            for m, y_acc in zip((1, 0), ys):
-                gated(g, m, y_acc)
-            for m in (1, 0):
-                target = windows[m][:].indirect(entries(g * P, (g + 1) * P))
-                nc.scalar.activation(target, y_gated[:, m, g * P : (g + 1) * P], COPY)
+            return {m: second(g, m, codes[:], scales[:]) for m in (1, 0)}
 
-        early_group(0, "h_bf0")
-        h3 = [side_product(0, "h_bf0")]
-        early_group(1, "w2_bf0")
-        h3.append(side_product(1, "w2_bf0"))
-        h2 = product(2, "gate0")
-        codes = sb("b_last1", [P, 2 * P], U32)
-        scales = sb("h_scales23", [P, 2 * P], U8)
-        quantise(codes[:, 0:P], scales[:, 0:P], h2)
-        for n in range(2):
-            part = slice(P + n * P // 2, P + (n + 1) * P // 2)
-            quantise(codes[:, part], scales[:, part], h3[n])
+        def scalar_scatter(g, m):
+            target = windows[m][:].indirect(entries(g * P, (g + 1) * P))
+            nc.scalar.activation(target, y_gated[m][:, place(g)], COPY)
+
+        def gate_both(g, y):
+            for m in (1, 0):
+                gated(g, m, y[m])
+
+        y0 = second_product(0, product(0, "h_bf0"))
+        h1 = product(1, "w2_bf0")
+        h2 = product(2, "h_bf2")
+        y1 = second_product(1, h1)
+        gate_both(0, y0)
+        y2 = second_product(2, h2)
+        h3 = product(3, "h_bf3")
+        gate_both(1, y1)
+        y3 = second_product(3, h3)
+        gate_both(2, y2)
+        for g in (0, 1):
+            for m in (1, 0):
+                scalar_scatter(g, m)
+        heads = {1: a_sb[3].rearrange("p n t -> p (n t)")[:, 0:HEAD], 0: sb("h_bf3", [P, HEAD], F32)[:]}
         for m in (1, 0):
-            head = sb("head%d" % m, [P, HEAD], F32)
-            nc.gpsimd.tensor_copy(head[:], windows[m][:, 0:HEAD])
-            nc.sync.dma_start(out[m * P : (m + 1) * P, 0:HEAD], head[:])
-        for m in (1, 0):
-            for g in (2, 3):
-                part = slice((g - 2) * P, (g - 1) * P)
-                gated(g, m, second(g, m, codes[:, part], scales[:, part]))
-        for g in (2, 3):
-            target = windows[1][:].indirect(entries(g * P, (g + 1) * P))
-            nc.scalar.activation(target, y_gated[:, 1, g * P : (g + 1) * P], COPY)
-        nc.vector.tensor_copy(windows[0][:].indirect(entries(HEAD, S)), y_gated[:, 0, HEAD:S])
+            nc.vector.tensor_copy(heads[m], windows[m][:, 0:HEAD])
+            nc.sync.dma_start(out[m * P : (m + 1) * P, 0:HEAD], heads[m])
+        gate_both(3, y3)
+        scalar_scatter(2, 1)
+        scalar_scatter(3, 1)
+        nc.vector.tensor_copy(windows[0][:].indirect(entries(HEAD, S)), y_gated[0][:, place(2, 2)])
         nc.scalar.dma_start(out[P : 2 * P, HEAD:T], windows[1][:, HEAD:T])
         nc.sync.dma_start(out[0:P, HEAD:T], windows[0][:, HEAD:T])

@@ -73,7 +73,10 @@ def tile_picked_depth_glu_relu_srt_p_kernel(
         w3_last = [
             load_rows("w3_last%d" % n, w3, PASSES - 1, slice(n * H // 2, (n + 1) * H // 2)) for n in range(2)
         ]
-        w2_raw = load_rows("w2_raw", w2, 0, slice(0, N))
+        w2_raw = sb("w2_raw", [P, PACK, N], F32)
+        w2_rows = w2.rearrange("(n u e v) c -> u n e (v c)", u=2, e=2, v=2)
+        for u in range(2):
+            nc.sync.dma_start(w2_raw[:, 2 * u : 2 * u + 2].rearrange("p v c -> p (v c)"), w2_rows[u])
         gate_sb = sb("gate_sb", [P, S], F32)
         nc.sync.dma_start(gate_sb[:], gate[0:P, :])
 
@@ -91,26 +94,24 @@ def tile_picked_depth_glu_relu_srt_p_kernel(
         x_planes = sb("x_planes", [P, S], U8)
         nc.vector.tensor_copy(x_planes[:], x_scale_rows[:].indirect(offsets[:]))
 
-        def deal(name, codes, scales, raw, first, plan):
-            src = raw[:].rearrange("p j (m t) -> p m j t", t=PACK)
-            for n, (engine, ts, ms) in enumerate(plan):
-                count = ms.stop - ms.start
-                grouped = sb("%s_bf%d" % (name, n), [P, ts.stop - ts.start, count, PACK], BF16)
-                cast(engine, grouped[:].rearrange("p t m j -> p m j t"), src[:, ms, :, ts])
+        def deal(name, codes, scales, raw, first, engines):
+            count = raw.shape[2] // PACK
+            src = raw[:].rearrange("p j (n u e v) -> p u n j e v", u=2, e=2, v=2)
+            for u, engine in enumerate(engines):
+                grouped = sb("%s_bf%d" % (name, u), [P, 2, count, PACK], BF16)
+                cast(engine, grouped[:].rearrange("p v (n e) j -> p n j e v", e=2), src[:, u])
                 if count == P:
+                    ts = slice(2 * u, 2 * u + 2)
                     quantise(
                         codes[:, ts, :].rearrange("p t m -> p (t m)"),
                         scales[:, ts, :].rearrange("p t m -> p (t m)"),
-                        grouped[:].rearrange("p t m j -> p (t m j)"),
+                        grouped[:].rearrange("p v m j -> p (v m j)"),
                     )
                 else:
-                    part = slice(first + ms.start, first + ms.stop)
-                    for t in range(ts.start, ts.stop):
-                        quantise(
-                            codes[:, t, part],
-                            scales[:, t, part],
-                            grouped[:, t - ts.start].rearrange("p m j -> p (m j)"),
-                        )
+                    part = slice(first, first + count)
+                    for v in range(2):
+                        t = 2 * u + v
+                        quantise(codes[:, t, part], scales[:, t, part], grouped[:, v].rearrange("p m j -> p (m j)"))
 
         def code_tiles(name):
             return sb(name + "_codes", [P, PACK, P], U32), sb(name + "_scales", [P, PACK, P], U8)
@@ -129,12 +130,8 @@ def tile_picked_depth_glu_relu_srt_p_kernel(
                         stop=(o == PASSES - 1 and t == PACK - 1),
                     )
 
-        low, high, every_t = slice(0, 2), slice(2, 4), slice(0, 4)
-        every_m, half_m, other_m = slice(0, P), slice(0, P // 2), slice(P // 2, P)
-        all_scalar = [("scalar", every_t, every_m)]
-        halves = [("vector", low, every_m), ("scalar", high, every_m)]
-        quarter = [("vector", low, every_m), ("vector", high, half_m), ("scalar", high, other_m)]
-        last_halves = [("vector", low, half_m), ("scalar", high, half_m)]
+        all_scalar = ("scalar", "scalar")
+        halves = ("vector", "scalar")
         order = range(GROUPS)
 
         a_acc = [bank(g, [P, PACK, P]) for g in range(GROUPS)]
@@ -145,27 +142,27 @@ def tile_picked_depth_glu_relu_srt_p_kernel(
 
         b_acc = [bank(GROUPS + g, [P, PACK, P]) for g in range(GROUPS)]
         codes, scales = code_tiles("w3_0")
-        deal("w3_0", codes, scales, w3_raw[0], 0, quarter)
+        deal("w3_0", codes, scales, w3_raw[0], 0, halves)
         first_pass(b_acc, 0, codes, scales, order)
 
         def interleaved(acc):
             return acc[:].rearrange("p t n -> p n t")
 
-        a_early = sb("w3_raw0", [P, 3, P, PACK], F32)
-        a_sb = [a_early[:, g] for g in range(GROUPS - 1)]
-        for g in range(GROUPS - 1):
-            nc.scalar.activation(a_sb[g], interleaved(a_acc[g]), RELU)
+        def rectify(g, dst):
+            nc.scalar.activation(dst, interleaved(a_acc[g]), RELU)
+            return dst
+
+        a_sb = [rectify(0, sb("w3_raw0", [P, P, PACK], F32)[:])]
 
         codes, scales = code_tiles("w3_1")
         deal("w3_1", codes, scales, w3_raw[1], 0, halves)
         first_pass(b_acc, 1, codes, scales, order)
         codes, scales = code_tiles("w3_2")
         for n in range(2):
-            deal("w3_last%d" % n, codes, scales, w3_last[n], n * P // 2, last_halves)
+            deal("w3_last%d" % n, codes, scales, w3_last[n], n * P // 2, halves)
         first_pass(b_acc, PASSES - 1, codes, scales, order)
 
-        a_sb.append(sb("w3_last1", [P, P, PACK], F32)[:])
-        nc.scalar.activation(a_sb[3], interleaved(a_acc[3]), RELU)
+        a_sb.append(rectify(1, sb("w3_last1", [P, P, PACK], F32)[:]))
 
         w2_codes = sb("w2_codes", [P, N], U32)
         w2_scales = sb("w2_scales", [P, N], U8)
@@ -178,6 +175,9 @@ def tile_picked_depth_glu_relu_srt_p_kernel(
                 w2_raw[:, :, cols].rearrange("p j (c i) -> p c j i", i=4),
             )
             quantise(w2_codes[:, cols], w2_scales[:, cols], w2_bf[:])
+
+        a_late = sb("w2_raw", [P, 2, P, PACK], F32)
+        a_sb.extend([rectify(2 + n, a_late[:, n]) for n in range(2)])
 
         y_gated = [sb("y_gated%d" % m, [P, 3 * P], F32) for m in range(N // P)]
 

@@ -13,7 +13,7 @@ U16 = mybir.dt.uint16
 U8 = mybir.dt.uint8
 FP8X4 = mybir.dt.float8_e4m3fn_x4
 MULT = mybir.AluOpType.mult
-RELU = mybir.ActivationFunctionType.Relu
+MAX = mybir.AluOpType.max
 COPY = mybir.ActivationFunctionType.Copy
 
 P = 128
@@ -61,17 +61,17 @@ def tile_picked_depth_glu_relu_srt_p_kernel(
         x_all = sb("x_all", [P, PASSES, T], U32)
         nc.sync.dma_start(x_all[:].bitcast(I32), x_words.rearrange("o p n t -> p o (n t)").bitcast(I32))
         nc.sync.dma_start(offsets[:], offs)
-        w1_raw = [load_rows("w1_raw0", w1, 0, whole)]
+        w3_raw = [load_rows("w3_raw0", w3, 0, whole)]
         for q in range(4):
             rows = slice(32 * q, 32 * q + 4 * PASSES)
             nc.sync.dma_start(
                 x_scale_rows[rows, :].bitcast(I32),
                 x_scales[:, 4 * q : 4 * q + 4, :].bitcast(I32),
             )
-        w1_raw.extend([load_rows("w1_raw%d" % o, w1, o, whole) for o in range(1, PASSES)])
-        w3_raw = [load_rows("w3_raw%d" % o, w3, o, whole) for o in range(PASSES - 1)]
-        w3_last = [
-            load_rows("w3_last%d" % n, w3, PASSES - 1, slice(n * H // 2, (n + 1) * H // 2)) for n in range(2)
+        w3_raw.extend([load_rows("w3_raw%d" % o, w3, o, whole) for o in range(1, PASSES)])
+        w1_raw = [load_rows("w1_raw%d" % o, w1, o, whole) for o in range(PASSES - 1)]
+        w1_last = [
+            load_rows("w1_last%d" % n, w1, PASSES - 1, slice(n * H // 2, (n + 1) * H // 2)) for n in range(2)
         ]
         w2_raw = sb("w2_raw", [P, PACK, N], F32)
         w2_rows = w2.rearrange("(n u e v) c -> u n e (v c)", u=2, e=2, v=2)
@@ -134,35 +134,35 @@ def tile_picked_depth_glu_relu_srt_p_kernel(
         halves = ("vector", "scalar")
         order = range(GROUPS)
 
-        a_acc = [bank(g, [P, PACK, P]) for g in range(GROUPS)]
+        b_acc = [bank(g, [P, PACK, P]) for g in range(GROUPS)]
         for o, plan in enumerate((all_scalar, halves, halves)):
-            codes, scales = code_tiles("w1_%d" % o)
-            deal("w1_%d" % o, codes, scales, w1_raw[o], 0, plan)
-            first_pass(a_acc, o, codes, scales, order)
+            codes, scales = code_tiles("w3_%d" % o)
+            deal("w3_%d" % o, codes, scales, w3_raw[o], 0, plan)
+            first_pass(b_acc, o, codes, scales, order)
 
-        b_acc = [bank(GROUPS + g, [P, PACK, P]) for g in range(GROUPS)]
-        codes, scales = code_tiles("w3_0")
-        deal("w3_0", codes, scales, w3_raw[0], 0, halves)
-        first_pass(b_acc, 0, codes, scales, order)
+        a_acc = [bank(GROUPS + g, [P, PACK, P]) for g in range(GROUPS)]
+        codes, scales = code_tiles("w1_0")
+        deal("w1_0", codes, scales, w1_raw[0], 0, halves)
+        first_pass(a_acc, 0, codes, scales, order)
 
         def interleaved(acc):
             return acc[:].rearrange("p t n -> p n t")
 
-        def rectify(g, dst):
-            nc.scalar.activation(dst, interleaved(a_acc[g]), RELU)
+        def empty_b(g, dst):
+            nc.scalar.copy(dst, interleaved(b_acc[g]))
             return dst
 
-        a_sb = [rectify(0, sb("w3_raw0", [P, P, PACK], F32)[:])]
+        b_sb = [empty_b(0, sb("w1_raw0", [P, P, PACK], F32)[:])]
 
-        codes, scales = code_tiles("w3_1")
-        deal("w3_1", codes, scales, w3_raw[1], 0, halves)
-        first_pass(b_acc, 1, codes, scales, order)
-        codes, scales = code_tiles("w3_2")
+        codes, scales = code_tiles("w1_1")
+        deal("w1_1", codes, scales, w1_raw[1], 0, halves)
+        first_pass(a_acc, 1, codes, scales, order)
+        codes, scales = code_tiles("w1_2")
         for n in range(2):
-            deal("w3_last%d" % n, codes, scales, w3_last[n], n * P // 2, halves)
-        first_pass(b_acc, PASSES - 1, codes, scales, order)
+            deal("w1_last%d" % n, codes, scales, w1_last[n], n * P // 2, halves)
+        first_pass(a_acc, PASSES - 1, codes, scales, order)
 
-        a_sb.append(rectify(1, sb("w3_last1", [P, P, PACK], F32)[:]))
+        b_sb.append(empty_b(1, sb("w1_last1", [P, P, PACK], F32)[:]))
 
         w2_codes = sb("w2_codes", [P, N], U32)
         w2_scales = sb("w2_scales", [P, N], U8)
@@ -176,8 +176,8 @@ def tile_picked_depth_glu_relu_srt_p_kernel(
             )
             quantise(w2_codes[:, cols], w2_scales[:, cols], w2_bf[:])
 
-        a_late = sb("w2_raw", [P, 2, P, PACK], F32)
-        a_sb.extend([rectify(2 + n, a_late[:, n]) for n in range(2)])
+        b_late = sb("w2_raw", [P, 2, P, PACK], F32)
+        b_sb.extend([empty_b(2 + n, b_late[:, n]) for n in range(2)])
 
         y_gated = [sb("y_gated%d" % m, [P, 3 * P], F32) for m in range(N // P)]
 
@@ -190,7 +190,7 @@ def tile_picked_depth_glu_relu_srt_p_kernel(
 
         def product(g, slot):
             grouped = sb(slot, [P, P, PACK], BF16)
-            nc.vector.tensor_tensor(grouped[:], interleaved(b_acc[g]), a_sb[g], MULT)
+            nc.vector.scalar_tensor_tensor(grouped[:], interleaved(a_acc[g]), 0.0, b_sb[g], MAX, MULT)
             return grouped[:].rearrange("p n t -> p (n t)")
 
         def second(g, m, codes, scales):
@@ -237,7 +237,7 @@ def tile_picked_depth_glu_relu_srt_p_kernel(
         for g in (0, 1):
             for m in (1, 0):
                 scalar_scatter(g, m)
-        heads = {1: a_sb[3].rearrange("p n t -> p (n t)")[:, 0:HEAD], 0: sb("h_bf3", [P, HEAD], F32)[:]}
+        heads = {1: b_sb[3].rearrange("p n t -> p (n t)")[:, 0:HEAD], 0: sb("h_bf3", [P, HEAD], F32)[:]}
         for m in (1, 0):
             nc.vector.tensor_copy(heads[m], windows[m][:, 0:HEAD])
             nc.sync.dma_start(out[m * P : (m + 1) * P, 0:HEAD], heads[m])

@@ -64,7 +64,7 @@ def tile_picked_depth_glu_relu_srt_p_kernel(
         w3_raw = [load_rows("w3_raw0", w3, 0, whole)]
         for q in range(4):
             rows = slice(32 * q, 32 * q + 4 * PASSES)
-            nc.sync.dma_start(
+            nc.scalar.dma_start(
                 x_scale_rows[rows, :].bitcast(I32),
                 x_scales[:, 4 * q : 4 * q + 4, :].bitcast(I32),
             )
@@ -94,11 +94,13 @@ def tile_picked_depth_glu_relu_srt_p_kernel(
         x_planes = sb("x_planes", [P, S], U8)
         nc.vector.tensor_copy(x_planes[:], x_scale_rows[:].indirect(offsets[:]))
 
+        shared = {("w3_1", 0): "w3_0_bf0"}
+
         def deal(name, codes, scales, raw, first, engines):
             count = raw.shape[2] // PACK
             src = raw[:].rearrange("p j (n u e v) -> p u n j e v", u=2, e=2, v=2)
             for u, engine in enumerate(engines):
-                grouped = sb("%s_bf%d" % (name, u), [P, 2, count, PACK], BF16)
+                grouped = sb(shared.get((name, u), "%s_bf%d" % (name, u)), [P, 2, count, PACK], BF16)
                 cast(engine, grouped[:].rearrange("p v (n e) j -> p n j e v", e=2), src[:, u])
                 if count == P:
                     ts = slice(2 * u, 2 * u + 2)
@@ -113,8 +115,8 @@ def tile_picked_depth_glu_relu_srt_p_kernel(
                         t = 2 * u + v
                         quantise(codes[:, t, part], scales[:, t, part], grouped[:, v].rearrange("p m j -> p (m j)"))
 
-        def code_tiles(name):
-            return sb(name + "_codes", [P, PACK, P], U32), sb(name + "_scales", [P, PACK, P], U8)
+        def code_tiles(name, scale_slot=None):
+            return sb(name + "_codes", [P, PACK, P], U32), sb(scale_slot or name + "_scales", [P, PACK, P], U8)
 
         def first_pass(acc, o, codes, scales, order):
             for g in order:
@@ -136,7 +138,7 @@ def tile_picked_depth_glu_relu_srt_p_kernel(
 
         b_acc = [bank(g, [P, PACK, P]) for g in range(GROUPS)]
         for o, plan in enumerate((all_scalar, halves, halves)):
-            codes, scales = code_tiles("w3_%d" % o)
+            codes, scales = code_tiles("w3_%d" % o, "x_scale_rows" if o == 0 else None)
             deal("w3_%d" % o, codes, scales, w3_raw[o], 0, plan)
             first_pass(b_acc, o, codes, scales, order)
 

@@ -30,6 +30,7 @@ def tile_picked_depth_glu_relu_srt_p_kernel(
     nc = tc.nc
     with ExitStack() as ctx:
         keep = ctx.enter_context(tc.tile_pool(name="keep", bufs=1))
+        late = ctx.enter_context(tc.tile_pool(name="late", bufs=1))
         psum = ctx.enter_context(tc.psum_pool(name="psum", bufs=1))
 
         def sb(name, shape, dtype):
@@ -51,6 +52,11 @@ def tile_picked_depth_glu_relu_srt_p_kernel(
         x_scale_rows = sb("x_scale_rows", [P, T], U8)
         nc.vector.memset(x_scale_rows[:].bitcast(I32), 0)
 
+        def load_x(o):
+            raw = sb("x_raw%d" % o, [P, T], U32)
+            nc.sync.dma_start(raw[:].bitcast(I32), x_words[o].rearrange("p n t -> p (n t)").bitcast(I32))
+            return raw
+
         def load_rows(name, w, o, cols):
             raw = sb(name, [P, PACK, cols.stop - cols.start], F32)
             rows = w[o * P * PACK : (o + 1) * P * PACK, cols]
@@ -58,25 +64,25 @@ def tile_picked_depth_glu_relu_srt_p_kernel(
             return raw
 
         whole = slice(0, H)
-        x_all = sb("x_all", [P, PASSES, T], U32)
-        nc.sync.dma_start(x_all[:].bitcast(I32), x_words.rearrange("o p n t -> p o (n t)").bitcast(I32))
+        x_raw = [load_x(0)]
         nc.sync.dma_start(offsets[:], offs)
-        w3_raw = [load_rows("w3_raw0", w3, 0, whole)]
+        x_raw.extend([load_x(o) for o in range(1, PASSES)])
         for q in range(4):
             rows = slice(32 * q, 32 * q + 4 * PASSES)
-            nc.scalar.dma_start(
+            queue = nc.sync if q < 2 else nc.scalar
+            queue.dma_start(
                 x_scale_rows[rows, :].bitcast(I32),
                 x_scales[:, 4 * q : 4 * q + 4, :].bitcast(I32),
             )
-        w3_raw.extend([load_rows("w3_raw%d" % o, w3, o, whole) for o in range(1, PASSES)])
+        w3_raw = [load_rows("w3_raw%d" % o, w3, o, whole) for o in range(PASSES)]
         w1_raw = [load_rows("w1_raw%d" % o, w1, o, whole) for o in range(PASSES - 1)]
         w1_last = [
             load_rows("w1_last%d" % n, w1, PASSES - 1, slice(n * H // 2, (n + 1) * H // 2)) for n in range(2)
         ]
-        w2_raw = sb("w2_raw", [P, PACK, N], F32)
-        w2_rows = w2.rearrange("(n u e v) c -> u n e (v c)", u=2, e=2, v=2)
-        for u in range(2):
-            nc.sync.dma_start(w2_raw[:, 2 * u : 2 * u + 2].rearrange("p v c -> p (v c)"), w2_rows[u])
+        w2_raw = late.tile([P, PACK, N], F32, name="w2_raw", align_bytes=64, offset=0)
+        w2_rows = w2.rearrange("(r t e) c -> t r e c", t=PACK, e=4)
+        for t in range(PACK):
+            nc.sync.dma_start(w2_raw[:, t, :], w2_rows[t])
         gate_sb = sb("gate_sb", [P, S], F32)
         nc.sync.dma_start(gate_sb[:], gate[0:P, :])
 
@@ -89,109 +95,122 @@ def tile_picked_depth_glu_relu_srt_p_kernel(
         x_codes = []
         for o in range(PASSES):
             picked = sb("x_codes%d" % o, [P, S], U32)
-            nc.vector.tensor_copy(picked[:], x_all[:, o, :].indirect(offsets[:]))
+            nc.vector.tensor_copy(picked[:], x_raw[o][:].indirect(offsets[:]))
             x_codes.append(picked)
         x_planes = sb("x_planes", [P, S], U8)
         nc.vector.tensor_copy(x_planes[:], x_scale_rows[:].indirect(offsets[:]))
 
-        shared = {("w3_1", 0): "w3_0_bf0"}
-
-        def deal(name, codes, scales, raw, first, engines):
+        def round_tiles(name, raw, engine, ts):
             count = raw.shape[2] // PACK
-            src = raw[:].rearrange("p j (n u e v) -> p u n j e v", u=2, e=2, v=2)
-            for u, engine in enumerate(engines):
-                grouped = sb(shared.get((name, u), "%s_bf%d" % (name, u)), [P, 2, count, PACK], BF16)
-                cast(engine, grouped[:].rearrange("p v (n e) j -> p n j e v", e=2), src[:, u])
-                if count == P:
-                    ts = slice(2 * u, 2 * u + 2)
-                    quantise(
-                        codes[:, ts, :].rearrange("p t m -> p (t m)"),
-                        scales[:, ts, :].rearrange("p t m -> p (t m)"),
-                        grouped[:].rearrange("p v m j -> p (v m j)"),
-                    )
-                else:
-                    part = slice(first, first + count)
-                    for v in range(2):
-                        t = 2 * u + v
-                        quantise(codes[:, t, part], scales[:, t, part], grouped[:, v].rearrange("p m j -> p (m j)"))
+            src = raw[:].rearrange("p j (r t e) -> p t r j e", t=PACK, e=4)
+            grouped = sb("%s_bf%d" % (name, ts.start), [P, ts.stop - ts.start, count, PACK], BF16)
+            cast(engine, grouped[:].rearrange("p t (r e) j -> p t r j e", e=4), src[:, ts])
+            return grouped
 
-        def code_tiles(name, scale_slot=None):
-            return sb(name + "_codes", [P, PACK, P], U32), sb(scale_slot or name + "_scales", [P, PACK, P], U8)
+        def deal_whole(name, raw, shares):
+            codes, scales = {}, {}
+            staged = [(ts, round_tiles(name, raw, engine, ts)) for engine, ts in shares]
+            for ts, grouped in staged:
+                width = (ts.stop - ts.start) * P
+                words = sb("%s_codes%d" % (name, ts.start), [P, width], U32)
+                planes = sb("%s_scales%d" % (name, ts.start), [P, width], U8)
+                quantise(words[:], planes[:], grouped[:].rearrange("p t m j -> p (t m j)"))
+                for t in range(ts.start, ts.stop):
+                    cols = slice((t - ts.start) * P, (t - ts.start + 1) * P)
+                    codes[t], scales[t] = words[:, cols], planes[:, cols]
+            return codes, scales
 
-        def first_pass(acc, o, codes, scales, order):
-            for g in order:
+        def deal_half(name, raw, codes, scales, first, shares, order):
+            part = slice(first, first + P // 2)
+            staged = {}
+            for engine, ts in shares:
+                grouped = round_tiles(name, raw, engine, ts)
+                for t in range(ts.start, ts.stop):
+                    staged[t] = grouped[:, t - ts.start].rearrange("p m j -> p (m j)")
+            for t in order:
+                quantise(codes[t][:, part], scales[t][:, part], staged[t])
+
+        def first_product(acc, o, codes, scales, steps):
+            seen = {g: 0 for g in range(GROUPS)}
+            for g, t in steps:
                 tokens = slice(g * P, (g + 1) * P)
-                for t in range(PACK):
-                    nc.tensor.matmul_mx(
-                        out=acc[g][:, t, :],
-                        lhsT=codes[:, t, :].bitcast(FP8X4),
-                        lhsT_scale=scales[:, t, :],
-                        rhs=x_codes[o][:, tokens].bitcast(FP8X4),
-                        rhs_scale=x_planes[4 * o : P, tokens],
-                        start=(o == 0 and t == 0),
-                        stop=(o == PASSES - 1 and t == PACK - 1),
-                    )
+                nc.tensor.matmul_mx(
+                    out=acc[g][:, t, :],
+                    lhsT=codes[t].bitcast(FP8X4),
+                    lhsT_scale=scales[t],
+                    rhs=x_codes[o][:, tokens].bitcast(FP8X4),
+                    rhs_scale=x_planes[4 * o : P, tokens],
+                    start=(o == 0 and seen[g] == 0),
+                    stop=(o == PASSES - 1 and seen[g] == PACK - 1),
+                )
+                seen[g] = seen[g] + 1
 
-        all_scalar = ("scalar", "scalar")
-        halves = ("vector", "scalar")
-        order = range(GROUPS)
+        halves = (("vector", slice(0, 2)), ("scalar", slice(2, 4)))
+
+        def by_share(shares):
+            return [(g, t) for engine, ts in shares for g in range(GROUPS) for t in range(ts.start, ts.stop)]
 
         b_acc = [bank(g, [P, PACK, P]) for g in range(GROUPS)]
-        for o, plan in enumerate((all_scalar, halves, halves)):
-            codes, scales = code_tiles("w3_%d" % o, "x_scale_rows" if o == 0 else None)
-            deal("w3_%d" % o, codes, scales, w3_raw[o], 0, plan)
-            first_pass(b_acc, o, codes, scales, order)
-
-        a_acc = [bank(GROUPS + g, [P, PACK, P]) for g in range(GROUPS)]
-        codes, scales = code_tiles("w1_0")
-        deal("w1_0", codes, scales, w1_raw[0], 0, halves)
-        first_pass(a_acc, 0, codes, scales, order)
+        for o in range(PASSES):
+            codes, scales = deal_whole("w3_%d" % o, w3_raw[o], halves)
+            first_product(b_acc, o, codes, scales, by_share(halves))
 
         def interleaved(acc):
             return acc[:].rearrange("p t n -> p n t")
 
         def empty_b(g, dst):
-            nc.scalar.copy(dst, interleaved(b_acc[g]))
-            return dst
+            nc.scalar.copy(dst[:], interleaved(b_acc[g]))
+            return dst[:]
 
-        b_sb = [empty_b(0, sb("w1_raw0", [P, P, PACK], F32)[:])]
+        a_acc = [bank(GROUPS + g, [P, PACK, P]) for g in range(GROUPS)]
+        three_one = (("vector", slice(0, 2)), ("scalar", slice(3, 4)), ("vector", slice(2, 3)))
+        codes, scales = deal_whole("w1_0", w1_raw[0], three_one)
+        first_product(a_acc, 0, codes, scales, by_share(three_one))
+        codes, scales = deal_whole("w1_1", w1_raw[1], halves)
+        first_product(a_acc, 1, codes, scales, by_share(halves))
+        b_sb = [empty_b(g, sb("b%d" % g, [P, P, PACK], F32)) for g in range(2)]
 
-        codes, scales = code_tiles("w1_1")
-        deal("w1_1", codes, scales, w1_raw[1], 0, halves)
-        first_pass(a_acc, 1, codes, scales, order)
-        codes, scales = code_tiles("w1_2")
-        for n in range(2):
-            deal("w1_last%d" % n, codes, scales, w1_last[n], n * P // 2, halves)
-        first_pass(a_acc, PASSES - 1, codes, scales, order)
-
-        b_sb.append(empty_b(1, sb("w1_last1", [P, P, PACK], F32)[:]))
+        codes = [sb("w1_2_codes%d" % t, [P, P], U32)[:] for t in range(PACK)]
+        scales = [sb("w1_2_scales%d" % t, [P, P], U8)[:] for t in range(PACK)]
+        deal_half("w1_last0", w1_last[0], codes, scales, 0, halves, range(PACK))
+        by_tile = (("scalar", slice(2, 3)), ("scalar", slice(3, 4)), ("vector", slice(0, 2)))
+        last_order = (2, 0, 1, 3)
+        deal_half("w1_last1", w1_last[1], codes, scales, P // 2, by_tile, last_order)
+        steps = [(g, t) for g in range(GROUPS) for t in last_order]
+        first_product(a_acc, PASSES - 1, codes, scales, steps)
+        b_sb.append(empty_b(2, sb("w1_last1", [P, P, PACK], F32)))
 
         w2_codes = sb("w2_codes", [P, N], U32)
         w2_scales = sb("w2_scales", [P, N], U8)
+        w2_bf = {}
         for m in (1, 0):
             cols = slice(m * P, (m + 1) * P)
-            w2_bf = sb("w2_bf%d" % m, [P, P * PACK], BF16)
-            cast(
-                "scalar" if m == 1 else "vector",
-                w2_bf[:].rearrange("p (c i j) -> p c j i", i=4, j=PACK),
+            w2_bf[m] = sb("w2_bf%d" % m, [P, P * PACK], BF16)
+            nc.scalar.copy(
+                w2_bf[m][:].rearrange("p (c i j) -> p c j i", i=4, j=PACK),
                 w2_raw[:, :, cols].rearrange("p j (c i) -> p c j i", i=4),
             )
-            quantise(w2_codes[:, cols], w2_scales[:, cols], w2_bf[:])
 
-        b_late = sb("w2_raw", [P, 2, P, PACK], F32)
-        b_sb.extend([empty_b(2 + n, b_late[:, n]) for n in range(2)])
+        b_sb.append(empty_b(3, late.tile([P, P, PACK], F32, name="b3", align_bytes=64, offset=0)))
 
-        y_gated = [sb("y_gated%d" % m, [P, 3 * P], F32) for m in range(N // P)]
+        def quantise_w2(m):
+            cols = slice(m * P, (m + 1) * P)
+            quantise(w2_codes[:, cols], w2_scales[:, cols], w2_bf[m][:])
 
-        def place(g, count=1):
-            first = (0, 2, 1, 2)[g] * P
-            return slice(first, first + count * P)
+        def y_gated(g, m, count=1):
+            if (g, m) in y_own:
+                return y_own[g, m]
+            first = (g % 2) * P
+            return y_lower[:, first : first + count * P]
 
         def entries(lo, hi):
             return offsets[:, lo // LIST_COL : hi // LIST_COL]
 
-        def product(g, slot):
-            grouped = sb(slot, [P, P, PACK], BF16)
+        def product(g):
+            if g == 2:
+                grouped = late.tile([P, P, PACK], BF16, name="h_bf2", align_bytes=64, offset=H * 4)
+            else:
+                grouped = sb("h_bf%d" % g, [P, P, PACK], BF16)
             nc.vector.scalar_tensor_tensor(grouped[:], interleaved(a_acc[g]), 0.0, b_sb[g], MAX, MULT)
             return grouped[:].rearrange("p n t -> p (n t)")
 
@@ -210,7 +229,7 @@ def tile_picked_depth_glu_relu_srt_p_kernel(
             return y_acc
 
         def gated(g, m, y_acc):
-            nc.vector.tensor_tensor(y_gated[m][:, place(g)], y_acc[:], gate_sb[:, g * P : (g + 1) * P], MULT)
+            nc.vector.tensor_tensor(y_gated(g, m), y_acc[:], gate_sb[:, g * P : (g + 1) * P], MULT)
 
         def second_product(g, h):
             codes = sb("h_codes%d" % g, [P, P], U32)
@@ -220,32 +239,44 @@ def tile_picked_depth_glu_relu_srt_p_kernel(
 
         def scalar_scatter(g, m):
             target = windows[m][:].indirect(entries(g * P, (g + 1) * P))
-            nc.scalar.activation(target, y_gated[m][:, place(g)], COPY)
+            nc.scalar.activation(target, y_gated(g, m), COPY)
 
-        def gate_both(g, y):
-            for m in (1, 0):
-                gated(g, m, y[m])
+        def store_head(m):
+            head = heads[:, m * HEAD : (m + 1) * HEAD]
+            nc.vector.tensor_copy(head, windows[m][:, 0:HEAD])
+            nc.sync.dma_start(out[m * P : (m + 1) * P, 0:HEAD], head)
 
-        y0 = second_product(0, product(0, "h_bf0"))
-        h1 = product(1, "w2_bf0")
-        h2 = product(2, "h_bf2")
+        h0 = product(0)
+        h1 = product(1)
+        quantise_w2(1)
+        quantise_w2(0)
+        y0 = second_product(0, h0)
         y1 = second_product(1, h1)
-        gate_both(0, y0)
+        h2 = product(2)
+        early = sb("w2_bf0", [P, 3 * P], F32)
+        y_own = {key: early[:, n * P : (n + 1) * P] for n, key in enumerate(((0, 1), (0, 0), (1, 1)))}
+        for g in (2, 3):
+            y_own[g, 1] = sb("y_upper%d" % g, [P, P], F32)[:]
+        gated(0, 1, y0[1])
+        gated(0, 0, y0[0])
+        gated(1, 1, y1[1])
         y2 = second_product(2, h2)
-        h3 = product(3, "h_bf3")
-        gate_both(1, y1)
+        h3 = product(3)
+        y_lower = late.tile([P, 2 * P], F32, name="y_lower", align_bytes=64, offset=H * 4)
+        gated(1, 0, y1[0])
         y3 = second_product(3, h3)
-        gate_both(2, y2)
         for g in (0, 1):
             for m in (1, 0):
                 scalar_scatter(g, m)
-        heads = {1: b_sb[3].rearrange("p n t -> p (n t)")[:, 0:HEAD], 0: sb("h_bf3", [P, HEAD], F32)[:]}
-        for m in (1, 0):
-            nc.vector.tensor_copy(heads[m], windows[m][:, 0:HEAD])
-            nc.sync.dma_start(out[m * P : (m + 1) * P, 0:HEAD], heads[m])
-        gate_both(3, y3)
+        heads = sb("heads", [P, 2 * HEAD], F32)
+        gated(2, 1, y2[1])
+        store_head(1)
+        gated(2, 0, y2[0])
+        gated(3, 1, y3[1])
+        store_head(0)
+        gated(3, 0, y3[0])
         scalar_scatter(2, 1)
         scalar_scatter(3, 1)
-        nc.vector.tensor_copy(windows[0][:].indirect(entries(HEAD, S)), y_gated[0][:, place(2, 2)])
+        nc.vector.tensor_copy(windows[0][:].indirect(entries(HEAD, S)), y_gated(2, 0, 2))
         nc.scalar.dma_start(out[P : 2 * P, HEAD:T], windows[1][:, HEAD:T])
         nc.sync.dma_start(out[0:P, HEAD:T], windows[0][:, HEAD:T])

@@ -278,5 +278,5 @@ def tile_picked_depth_glu_relu_srt_p_kernel(
         scalar_scatter(2, 1)
         scalar_scatter(3, 1)
         nc.vector.tensor_copy(windows[0][:].indirect(entries(HEAD, S)), y_gated(2, 0, 2))
-        nc.scalar.dma_start(out[P : 2 * P, HEAD:T], windows[1][:, HEAD:T])
+        nc.sync.dma_start(out[P : 2 * P, HEAD:T], windows[1][:, HEAD:T])
         nc.sync.dma_start(out[0:P, HEAD:T], windows[0][:, HEAD:T])

@@ -67,14 +67,19 @@ def tile_picked_depth_glu_relu_srt_p_kernel(
         x_raw = [load_x(0)]
         nc.sync.dma_start(offsets[:], offs)
         x_raw.extend([load_x(o) for o in range(1, PASSES)])
-        for q in range(4):
+
+        def load_scale_rows(q):
             rows = slice(32 * q, 32 * q + 4 * PASSES)
-            queue = nc.sync if q < 2 else nc.scalar
-            queue.dma_start(
+            nc.sync.dma_start(
                 x_scale_rows[rows, :].bitcast(I32),
                 x_scales[:, 4 * q : 4 * q + 4, :].bitcast(I32),
             )
-        w3_raw = [load_rows("w3_raw%d" % o, w3, o, whole) for o in range(PASSES)]
+
+        for q in range(3):
+            load_scale_rows(q)
+        w3_raw = [load_rows("w3_raw0", w3, 0, whole)]
+        load_scale_rows(3)
+        w3_raw.extend([load_rows("w3_raw%d" % o, w3, o, whole) for o in range(1, PASSES)])
         w1_raw = [load_rows("w1_raw%d" % o, w1, o, whole) for o in range(PASSES - 1)]
         w1_last = [
             load_rows("w1_last%d" % n, w1, PASSES - 1, slice(n * H // 2, (n + 1) * H // 2)) for n in range(2)

@@ -237,7 +237,10 @@ def tile_picked_depth_glu_relu_srt_p_kernel(
             nc.vector.tensor_tensor(y_gated(g, m), y_acc[:], gate_sb[:, g * P : (g + 1) * P], MULT)
 
         def second_product(g, h):
-            codes = sb("h_codes%d" % g, [P, P], U32)
+            if g == 1:
+                codes = late.tile([P, P], U32, name="h_codes1", align_bytes=64, offset=H * 6)
+            else:
+                codes = sb("h_codes%d" % g, [P, P], U32)
             scales = sb("h_scales%d" % g, [P, P], U8)
             quantise(codes[:], scales[:], h)
             return {m: second(g, m, codes[:], scales[:]) for m in (1, 0)}

from contextlib import ExitStack

import concourse.mybir as mybir

K, T, S, H, N = 1536, 1024, 512, 512, 256
FLOPS = 2 * S * (2 * K * H + H * N)

F32 = mybir.dt.float32
BF16 = mybir.dt.bfloat16
I32 = mybir.dt.int32
U32 = mybir.dt.uint32
U16 = mybir.dt.uint16
U8 = mybir.dt.uint8
FP8X4 = mybir.dt.float8_e4m3fn_x4
MULT = mybir.AluOpType.mult
MAX = mybir.AluOpType.max
COPY = mybir.ActivationFunctionType.Copy

P = 128
PACK = 4
PASSES = K // (P * PACK)
GROUPS = S // P
LIST_COL = 16
HEAD = S // 2


def tile_picked_depth_glu_relu_srt_p_kernel(
    tc, x_words, x_scales, w1, w3, w2, gate, offs, out
):
    nc = tc.nc
    with ExitStack() as ctx:
        keep = ctx.enter_context(tc.tile_pool(name="keep", bufs=1))
        late = ctx.enter_context(tc.tile_pool(name="late", bufs=1))
        psum = ctx.enter_context(tc.psum_pool(name="psum", bufs=1))

        def sb(name, shape, dtype):
            return keep.tile(shape, dtype, name=name, align_bytes=64)

        def bank(b, shape):
            return psum.tile(shape, F32, name="bank%d" % b)

        def quantise(codes, scales, grouped):
            nc.vector.quantize_mx(out=codes.bitcast(FP8X4), scales=scales, in_=grouped)

        def cast(engine, dst, src):
            if engine == "scalar":
                nc.scalar.copy(dst, src)
            else:
                nc.vector.tensor_copy(dst, src)

        offsets = keep.tile([P, S // LIST_COL], U16, name="offsets")
        x_scale_rows = sb("x_scale_rows", [P, T], U8)
        nc.vector.memset(x_scale_rows[:].bitcast(I32), 0)

        def load_x(o):
            raw = sb("x_raw%d" % o, [P, T], U32)
            nc.sync.dma_start(raw[:].bitcast(I32), x_words[o].rearrange("p n t -> p (n t)").bitcast(I32))
            return raw

        def load_rows(name, w, o, cols):
            raw = sb(name, [P, PACK, cols.stop - cols.start], F32)
            rows = w[o * P * PACK : (o + 1) * P * PACK, cols]
            nc.sync.dma_start(raw[:], rows.rearrange("(p j) c -> p j c", j=PACK))
            return raw

        whole = slice(0, H)
        x_raw = [load_x(0)]
        nc.sync.dma_start(offsets[:], offs)
        x_raw.extend([load_x(o) for o in range(1, PASSES)])

        def load_scale_rows(q):
            rows = slice(32 * q, 32 * q + 4 * PASSES)
            nc.sync.dma_start(
                x_scale_rows[rows, :].bitcast(I32),
                x_scales[:, 4 * q : 4 * q + 4, :].bitcast(I32),
            )

        for q in range(3):
            load_scale_rows(q)
        w3_raw = [load_rows("w3_raw0", w3, 0, whole)]
        load_scale_rows(3)
        w3_raw.extend([load_rows("w3_raw%d" % o, w3, o, whole) for o in range(1, PASSES)])
        w1_raw = [load_rows("w1_raw%d" % o, w1, o, whole) for o in range(PASSES - 1)]
        w1_last = [
            load_rows("w1_last%d" % n, w1, PASSES - 1, slice(n * H // 2, (n + 1) * H // 2)) for n in range(2)
        ]
        w2_raw = late.tile([P, PACK, N], F32, name="w2_raw", align_bytes=64, offset=0)
        w2_rows = w2.rearrange("(r t e) c -> t r e c", t=PACK, e=4)
        for t in range(PACK):
            nc.sync.dma_start(w2_raw[:, t, :], w2_rows[t])
        gate_sb = sb("gate_sb", [P, S], F32)
        nc.sync.dma_start(gate_sb[:], gate[0:P, :])

        windows = []
        for m in range(N // P):
            window = sb("window%d" % m, [P, T], F32)
            nc.vector.memset(window[:], 0.0)
            windows.append(window)

        x_codes = []
        for o in range(PASSES):
            picked = sb("x_codes%d" % o, [P, S], U32)
            nc.vector.tensor_copy(picked[:], x_raw[o][:].indirect(offsets[:]))
            x_codes.append(picked)
        x_planes = sb("x_planes", [P, S], U8)
        nc.vector.tensor_copy(x_planes[:], x_scale_rows[:].indirect(offsets[:]))

        def round_tiles(name, raw, engine, ts):
            count = raw.shape[2] // PACK
            src = raw[:].rearrange("p j (r t e) -> p t r j e", t=PACK, e=4)
            grouped = sb("%s_bf%d" % (name, ts.start), [P, ts.stop - ts.start, count, PACK], BF16)
            cast(engine, grouped[:].rearrange("p t (r e) j -> p t r j e", e=4), src[:, ts])
            return grouped

        def deal_whole(name, raw, shares):
            codes, scales = {}, {}
            staged = [(ts, round_tiles(name, raw, engine, ts)) for engine, ts in shares]
            for ts, grouped in staged:
                width = (ts.stop - ts.start) * P
                words = sb("%s_codes%d" % (name, ts.start), [P, width], U32)
                planes = sb("%s_scales%d" % (name, ts.start), [P, width], U8)
                quantise(words[:], planes[:], grouped[:].rearrange("p t m j -> p (t m j)"))
                for t in range(ts.start, ts.stop):
                    cols = slice((t - ts.start) * P, (t - ts.start + 1) * P)
                    codes[t], scales[t] = words[:, cols], planes[:, cols]
            return codes, scales

        def deal_half(name, raw, codes, scales, first, shares, order):
            part = slice(first, first + P // 2)
            staged = {}
            for engine, ts in shares:
                grouped = round_tiles(name, raw, engine, ts)
                for t in range(ts.start, ts.stop):
                    staged[t] = grouped[:, t - ts.start].rearrange("p m j -> p (m j)")
            for t in order:
                quantise(codes[t][:, part], scales[t][:, part], staged[t])

        def first_product(acc, o, codes, scales, steps):
            seen = {g: 0 for g in range(GROUPS)}
            for g, t in steps:
                tokens = slice(g * P, (g + 1) * P)
                nc.tensor.matmul_mx(
                    out=acc[g][:, t, :],
                    lhsT=codes[t].bitcast(FP8X4),
                    lhsT_scale=scales[t],
                    rhs=x_codes[o][:, tokens].bitcast(FP8X4),
                    rhs_scale=x_planes[4 * o : P, tokens],
                    start=(o == 0 and seen[g] == 0),
                    stop=(o == PASSES - 1 and seen[g] == PACK - 1),
                )
                seen[g] = seen[g] + 1

        halves = (("vector", slice(0, 2)), ("scalar", slice(2, 4)))

        def by_share(shares):
            return [(g, t) for engine, ts in shares for g in range(GROUPS) for t in range(ts.start, ts.stop)]

        b_acc = [bank(g, [P, PACK, P]) for g in range(GROUPS)]
        for o in range(PASSES):
            codes, scales = deal_whole("w3_%d" % o, w3_raw[o], halves)
            first_product(b_acc, o, codes, scales, by_share(halves))

        def interleaved(acc):
            return acc[:].rearrange("p t n -> p n t")

        def empty_b(g, dst):
            nc.scalar.copy(dst[:], interleaved(b_acc[g]))
            return dst[:]

        a_acc = [bank(GROUPS + g, [P, PACK, P]) for g in range(GROUPS)]
        three_one = (("vector", slice(0, 2)), ("scalar", slice(3, 4)), ("vector", slice(2, 3)))
        codes, scales = deal_whole("w1_0", w1_raw[0], three_one)
        first_product(a_acc, 0, codes, scales, by_share(three_one))
        codes, scales = deal_whole("w1_1", w1_raw[1], halves)
        first_product(a_acc, 1, codes, scales, by_share(halves))
        b_sb = [empty_b(g, sb("b%d" % g, [P, P, PACK], F32)) for g in range(2)]

        codes = [sb("w1_2_codes%d" % t, [P, P], U32)[:] for t in range(PACK)]
        scales = [sb("w1_2_scales%d" % t, [P, P], U8)[:] for t in range(PACK)]
        deal_half("w1_last0", w1_last[0], codes, scales, 0, halves, range(PACK))
        by_tile = (("scalar", slice(2, 3)), ("scalar", slice(3, 4)), ("vector", slice(0, 2)))
        last_order = (2, 0, 1, 3)
        deal_half("w1_last1", w1_last[1], codes, scales, P // 2, by_tile, last_order)
        steps = [(g, t) for g in range(GROUPS) for t in last_order]
        first_product(a_acc, PASSES - 1, codes, scales, steps)
        b_sb.append(empty_b(2, sb("w1_last1", [P, P, PACK], F32)))

        w2_codes = sb("w2_codes", [P, N], U32)
        w2_scales = sb("w2_scales", [P, N], U8)
        w2_bf = {}
        for m in (1, 0):
            cols = slice(m * P, (m + 1) * P)
            w2_bf[m] = sb("w2_bf%d" % m, [P, P * PACK], BF16)
            nc.scalar.copy(
                w2_bf[m][:].rearrange("p (c i j) -> p c j i", i=4, j=PACK),
                w2_raw[:, :, cols].rearrange("p j (c i) -> p c j i", i=4),
            )

        b_sb.append(empty_b(3, late.tile([P, P, PACK], F32, name="b3", align_bytes=64, offset=0)))

        def quantise_w2(m):
            cols = slice(m * P, (m + 1) * P)
            quantise(w2_codes[:, cols], w2_scales[:, cols], w2_bf[m][:])

        def y_gated(g, m, count=1):
            if (g, m) in y_own:
                return y_own[g, m]
            first = (g % 2) * P
            return y_lower[:, first : first + count * P]

        def entries(lo, hi):
            return offsets[:, lo // LIST_COL : hi // LIST_COL]

        def product(g):
            if g == 2:
                grouped = late.tile([P, P, PACK], BF16, name="h_bf2", align_bytes=64, offset=H * 4)
            else:
                grouped = sb("h_bf%d" % g, [P, P, PACK], BF16)
            nc.vector.scalar_tensor_tensor(grouped[:], interleaved(a_acc[g]), 0.0, b_sb[g], MAX, MULT)
            return grouped[:].rearrange("p n t -> p (n t)")

        def second(g, m, codes, scales):
            cols = slice(m * P, (m + 1) * P)
            y_acc = bank(g if m == 1 else GROUPS + g, [P, P])
            nc.tensor.matmul_mx(
                out=y_acc[:],
                lhsT=w2_codes[:, cols].bitcast(FP8X4),
                lhsT_scale=w2_scales[:, cols],
                rhs=codes.bitcast(FP8X4),
                rhs_scale=scales,
                start=True,
                stop=True,
            )
            return y_acc

        def gated(g, m, y_acc):
            nc.vector.tensor_tensor(y_gated(g, m), y_acc[:], gate_sb[:, g * P : (g + 1) * P], MULT)

        def second_product(g, h):
            if g == 1:
                codes = late.tile([P, P], U32, name="h_codes1", align_bytes=64, offset=H * 6)
            else:
                codes = sb("h_codes%d" % g, [P, P], U32)
            scales = sb("h_scales%d" % g, [P, P], U8)
            quantise(codes[:], scales[:], h)
            return {m: second(g, m, codes[:], scales[:]) for m in (1, 0)}

        def scalar_scatter(g, m):
            target = windows[m][:].indirect(entries(g * P, (g + 1) * P))
            nc.scalar.activation(target, y_gated(g, m), COPY)

        def store_head(m):
            head = heads[:, m * HEAD : (m + 1) * HEAD]
            nc.vector.tensor_copy(head, windows[m][:, 0:HEAD])
            nc.sync.dma_start(out[m * P : (m + 1) * P, 0:HEAD], head)

        h0 = product(0)
        h1 = product(1)
        quantise_w2(1)
        quantise_w2(0)
        y0 = second_product(0, h0)
        y1 = second_product(1, h1)
        h2 = product(2)
        early = sb("w2_bf0", [P, 3 * P], F32)
        y_own = {key: early[:, n * P : (n + 1) * P] for n, key in enumerate(((0, 1), (0, 0), (1, 1)))}
        for g in (2, 3):
            y_own[g, 1] = sb("y_upper%d" % g, [P, P], F32)[:]
        gated(0, 1, y0[1])
        gated(0, 0, y0[0])
        gated(1, 1, y1[1])
        y2 = second_product(2, h2)
        h3 = product(3)
        y_lower = late.tile([P, 2 * P], F32, name="y_lower", align_bytes=64, offset=H * 4)
        gated(1, 0, y1[0])
        y3 = second_product(3, h3)
        for g in (0, 1):
            for m in (1, 0):
                scalar_scatter(g, m)
        heads = sb("heads", [P, 2 * HEAD], F32)
        gated(2, 1, y2[1])
        store_head(1)
        gated(2, 0, y2[0])
        gated(3, 1, y3[1])
        store_head(0)
        gated(3, 0, y3[0])
        scalar_scatter(2, 1)
        scalar_scatter(3, 1)
        nc.vector.tensor_copy(windows[0][:].indirect(entries(HEAD, S)), y_gated(2, 0, 2))
        nc.sync.dma_start(out[P : 2 * P, HEAD:T], windows[1][:, HEAD:T])
        nc.sync.dma_start(out[0:P, HEAD:T], windows[0][:, HEAD:T])
